import numpy as np
import ml_dtypes


def mxq(x, axis, fmt="e4m3"):
    dtype, down = {"e4m3": (ml_dtypes.float8_e4m3fn, 7), "e5m2": (ml_dtypes.float8_e5m2, 14)}[fmt]
    v = np.moveaxis(np.asarray(x, np.float32).astype(ml_dtypes.bfloat16).astype(np.float64), axis, -1)
    blocks = v.reshape(v.shape[:-1] + (-1, 32))
    amax = np.abs(blocks).max(-1, keepdims=True)
    byte = np.maximum(np.where(amax > 0, np.frexp(amax)[1] - 1 + 127, 0) - down, 1)
    scale = np.exp2(byte - 127.0)
    codes = (blocks / scale).astype(np.float32).astype(dtype).astype(np.float64)
    return np.moveaxis((codes * scale).reshape(v.shape), -1, axis)


WIDE = False


def mx_kscale(k):
    if not WIDE:
        return np.ones(k)
    levels = np.array([10, -10, 5, -5, 0])
    if k % 512:
        return np.exp2(np.random.permutation(np.resize(levels, k // 32))).repeat(32)
    a = np.empty((k // 512, 16))
    for p in range(k // 512):
        a[p, :8] = np.random.permutation(np.resize(levels, 8))
        for g in range(8):
            far = levels[np.abs(levels - a[p, g]) >= 10]
            a[p, g + 8] = far[np.random.randint(len(far))]
    return np.exp2(a.ravel()).repeat(32)


def f64(x):
    return np.asarray(x).astype(np.float64)


def striped(idx):
    return np.tile(idx.reshape(-1, 16).T, (8, 1)).astype(np.uint16)


def unstriped(offs):
    return offs[:16].T.reshape(-1).astype(np.int64)


E2M1 = np.array([0.0, 0.5, 1.0, 1.5, 2.0, 3.0, 4.0, 6.0, -0.0, -0.5, -1.0, -1.5, -2.0, -3.0, -4.0, -6.0])


def pack_fp4(w):
    k, n = w.shape
    w = f64(np.asarray(w, np.float32).astype(ml_dtypes.bfloat16)).reshape(k // 32, 32, n)
    amax = np.abs(w).max(1)
    mant, ex = np.frexp(amax / 6.0)
    byte = np.clip(np.where(amax > 0, np.where(mant > 0.5, ex, ex - 1) + 127, 1), 1, 254)
    scaled = (w * np.exp2(127.0 - byte)[:, None, :]).reshape(k, n).astype(np.float32)
    c = np.ascontiguousarray(scaled.reshape(k // 512, 128, 4, n).transpose(0, 1, 3, 2)).astype(ml_dtypes.float4_e2m1fn).view(np.uint8) & 0xF
    words = (c[..., 0::2] | (c[..., 1::2] << 4)).reshape(k // 512, 128, 2 * n)
    return np.ascontiguousarray(words), np.ascontiguousarray(byte.astype(np.uint8).reshape(k // 512, 16, n))


def unpack_fp4(words, scales):
    g, _, n = scales.shape
    words = np.ascontiguousarray(words).reshape(g, 128, n, 2)
    nib = np.empty((g, 128, n, 4), np.uint8)
    nib[..., 0::2] = words & 0xF
    nib[..., 1::2] = words >> 4
    vals = E2M1[nib] * np.repeat(np.exp2(scales.astype(np.float64) - 127.0), 8, axis=1)[..., None]
    return vals.transpose(0, 1, 3, 2).reshape(g * 512, n)


def relu(v):
    return np.maximum(v, 0.0)


def sigmoid(v):
    return 1.0 / (1.0 + np.exp(-np.maximum(v, -700.0)))


K, T, S, N = 1024, 1024, 512, 128


def setup_inputs():
    n = np.random.standard_normal
    s = mx_kscale(K)[:, None]
    packed_w1 = pack_fp4(n((K, N)) / np.sqrt(K) / s)
    packed_w2 = pack_fp4(n((K, N)) / np.sqrt(K) / s)
    return {
        "xT": (n((K, T)) * s).astype(np.float32),
        "res": n((N, T)).astype(np.float32),
        "w1_words": packed_w1[0],
        "w1_scales": packed_w1[1],
        "w2_words": packed_w2[0],
        "w2_scales": packed_w2[1],
        "offs": striped(np.random.permutation(T)[:S]),
    }


def reference(xT, res, w1_words, w1_scales, w2_words, w2_scales, offs):
    r = f64(res)[:, unstriped(offs)]
    xq = mxq(f64(xT)[:, unstriped(offs)], 0, "e4m3")
    g = sigmoid(unpack_fp4(w2_words, w2_scales).T @ xq)
    y = relu(unpack_fp4(w1_words, w1_scales).T @ xq)
    return r + g * (y - r)

@@ -1,0 +1,135 @@
+from contextlib import ExitStack
+
+import concourse.mybir as mybir
+
+K, T, S, N = 1024, 1024, 512, 128
+FLOPS = 2 * 2 * K * S * N
+
+F32 = mybir.dt.float32
+BF16 = mybir.dt.bfloat16
+I32 = mybir.dt.int32
+U32 = mybir.dt.uint32
+U16 = mybir.dt.uint16
+U8 = mybir.dt.uint8
+FP8X4 = mybir.dt.float8_e4m3fn_x4
+FP4X4 = mybir.dt.float4_e2m1fn_x4
+ALU = mybir.AluOpType
+SIGMOID = mybir.ActivationFunctionType.Sigmoid
+
+P = 128
+PASSES = K // 512
+HALF = T // 2
+CHUNK = 128
+CHUNKS = S // CHUNK
+SCALAR_COLS = 256
+SCALAR_COLS_LAST = 160
+
+
+def tile_picked_highway_relu_l_kernel(tc, xT, res, w1_words, w1_scales, w2_words, w2_scales, offs, out):
+    nc = tc.nc
+    with ExitStack() as ctx:
+        keep = ctx.enter_context(tc.tile_pool(name="keep", bufs=1))
+        psum = ctx.enter_context(tc.psum_pool(name="psum", bufs=1))
+
+        offsets = keep.tile([P, S // 16], U16, name="offsets")
+        warm = keep.tile([P, 8], F32, name="warm")
+        warm_out = keep.tile([P, 8], F32, name="warm_out")
+        nc.vector.memset(warm[:], 0.0)
+        nc.scalar.activation(warm_out[:], warm[:], SIGMOID)
+
+        w_scales = keep.tile([P, 2, PASSES, N], U8, name="w_scales", align_bytes=64)
+        nc.gpsimd.memset(w_scales[:].rearrange("p w z c -> p (w z c)").bitcast(I32), 0)
+        for w, scales in enumerate((w1_scales, w2_scales)):
+            rows = scales.rearrange("z (q r) c -> r q z c", r=4)
+            for r in range(4):
+                nc.gpsimd.dma_start(out=w_scales[r:P:32, w, :, :].bitcast(I32), in_=rows[r].bitcast(I32))
+
+        raw = {}
+
+        def load_x(z, u, h):
+            raw[z, u, h] = keep.tile([P, 2, HALF], F32, name="raw_%d_%d_%d" % (z, u, h))
+            rows = xT[512 * z : 512 * (z + 1), :].rearrange("(p j) c -> p j c", j=4)
+            nc.sync.dma_start(out=raw[z, u, h][:], in_=rows[:, 2 * u : 2 * u + 2, h * HALF : (h + 1) * HALF])
+
+        load_x(0, 0, 0)
+        nc.sync.dma_start(offsets[:], offs)
+        load_x(0, 0, 1)
+        res_sb = keep.tile([P, T], F32, name="res_sb")
+        nc.sync.dma_start(out=res_sb[:], in_=res)
+        for z, u in ((0, 1), (1, 0), (1, 1)):
+            for h in range(2):
+                load_x(z, u, h)
+        w_words = []
+        for w, words in enumerate((w1_words, w2_words)):
+            w_words.append(keep.tile([P, PASSES, 2 * N], U8, name="w_words%d" % w, align_bytes=64))
+            nc.sync.dma_start(out=w_words[w][:].bitcast(I32), in_=words.rearrange("z p b -> p z b").bitcast(I32))
+
+        def cast_pair(z, u):
+            window = keep.tile([P, T], U32, name="window_%d_%d" % (z, u))
+            pairs = window[:].bitcast(BF16).rearrange("p (c e) -> p c e", e=2)
+            for h in range(2):
+                cut = SCALAR_COLS_LAST if (z, u, h) == (1, 1, 1) else SCALAR_COLS
+                src = raw[z, u, h][:].rearrange("p e c -> p c e")
+                nc.scalar.copy(pairs[:, h * HALF : h * HALF + cut, :], src[:, 0:cut, :])
+                nc.vector.tensor_copy(pairs[:, h * HALF + cut : (h + 1) * HALF, :], src[:, cut:HALF, :])
+            return window
+
+        picked0 = keep.tile([P, 2, S], U32, name="picked0")
+        window = cast_pair(0, 0)
+        nc.vector.tensor_copy(picked0[:, 0, :], window[:].indirect(offsets[:]))
+        r_picked = keep.tile([P, S], F32, name="r_picked")
+        nc.vector.tensor_copy(r_picked[:], res_sb[:].indirect(offsets[:]))
+        window = cast_pair(0, 1)
+        nc.vector.tensor_copy(picked0[:, 1, :], window[:].indirect(offsets[:]))
+        woven0 = keep.tile([P, 4 * S], BF16, name="woven0", align_bytes=64)
+        nc.vector.tensor_copy(
+            woven0[:].bitcast(I32).rearrange("p (c u) -> p c u", u=2),
+            picked0[:].bitcast(I32).rearrange("p u c -> p c u"),
+        )
+        codes0 = keep.tile([P, S], U32, name="codes0", align_bytes=64)
+        scales0 = keep.tile([P, S], U8, name="scales0", align_bytes=64)
+        nc.vector.quantize_mx(out=codes0[:].bitcast(FP8X4), scales=scales0[:], in_=woven0[:])
+
+        picked1 = [keep.tile([P, 2, CHUNK], U32, name="picked1_%d" % c) for c in range(CHUNKS)]
+        for u in range(2):
+            window = cast_pair(1, u)
+            for c in range(CHUNKS):
+                piece = offsets[:, c * CHUNK // 16 : (c + 1) * CHUNK // 16]
+                nc.vector.tensor_copy(picked1[c][:, u, :], window[:].indirect(piece))
+
+        codes1, scales1 = [], []
+        for c in range(CHUNKS):
+            woven1 = keep.tile([P, 4 * CHUNK], BF16, name="woven1_%d" % c, align_bytes=64)
+            nc.scalar.copy(
+                woven1[:].bitcast(U32).rearrange("p (c u) -> p c u", u=2),
+                picked1[c][:].rearrange("p u c -> p c u"),
+            )
+            codes1.append(keep.tile([P, CHUNK], U32, name="codes1_%d" % c, align_bytes=64))
+            scales1.append(keep.tile([P, CHUNK], U8, name="scales1_%d" % c, align_bytes=64))
+            nc.vector.quantize_mx(out=codes1[c][:].bitcast(FP8X4), scales=scales1[c][:], in_=woven1[:])
+
+        for c in range(CHUNKS):
+            cols = slice(c * CHUNK, (c + 1) * CHUNK)
+            sums = []
+            for w in (1, 0):
+                acc = psum.tile([N, CHUNK], F32, name="acc_%d_%d" % (w, c))
+                sums.append(acc)
+                for z in range(PASSES):
+                    nc.tensor.matmul_mx(
+                        out=acc[:],
+                        lhsT=w_words[w][:, z, :].bitcast(FP4X4),
+                        lhsT_scale=w_scales[:, w, z, :],
+                        rhs=(codes0[:, cols] if z == 0 else codes1[c][:]).bitcast(FP8X4),
+                        rhs_scale=scales0[:, cols] if z == 0 else scales1[c][:],
+                        start=(z == 0),
+                        stop=(z == PASSES - 1),
+                    )
+            gate = keep.tile([N, CHUNK], F32, name="gate%d" % c)
+            nc.scalar.activation(gate[:], sums[0][:], SIGMOID)
+            diff = keep.tile([N, CHUNK], F32, name="diff%d" % c)
+            nc.vector.scalar_tensor_tensor(diff[:], sums[1][:], 0.0, r_picked[:, cols], ALU.max, ALU.subtract)
+            gated = keep.tile([N, CHUNK], F32, name="gated%d" % c)
+            nc.vector.tensor_tensor(gated[:], diff[:], gate[:], ALU.mult)
+            result = keep.tile([N, CHUNK], F32, name="result%d" % c)
+            nc.vector.tensor_tensor(result[:], gated[:], r_picked[:, cols], ALU.add)
+            nc.sync.dma_start(out=out[:, cols], in_=result[:])

@@ -21,8 +21,8 @@ PASSES = K // 512
 HALF = T // 2
 CHUNK = 128
 CHUNKS = S // CHUNK
-SCALAR_COLS = 256
-SCALAR_COLS_LAST = 160
+SCALAR_COLUMNS = 176
+LAYER, GATE = 0, 1
 
 
 def tile_picked_highway_relu_l_kernel(tc, xT, res, w1_words, w1_scales, w2_words, w2_scales, offs, out):
@@ -32,104 +32,131 @@ def tile_picked_highway_relu_l_kernel(tc, xT, res, w1_words, w1_scales, w2_words
         psum = ctx.enter_context(tc.psum_pool(name="psum", bufs=1))
 
         offsets = keep.tile([P, S // 16], U16, name="offsets")
+        w_scales = [keep.tile([P, PASSES, N], U8, name="w_scales%d" % w, align_bytes=64) for w in (LAYER, GATE)]
+        for w in (LAYER, GATE):
+            nc.gpsimd.memset(w_scales[w][:].rearrange("p z c -> p (z c)").bitcast(I32), 0)
         warm = keep.tile([P, 8], F32, name="warm")
         warm_out = keep.tile([P, 8], F32, name="warm_out")
         nc.vector.memset(warm[:], 0.0)
         nc.scalar.activation(warm_out[:], warm[:], SIGMOID)
 
-        w_scales = keep.tile([P, 2, PASSES, N], U8, name="w_scales", align_bytes=64)
-        nc.gpsimd.memset(w_scales[:].rearrange("p w z c -> p (w z c)").bitcast(I32), 0)
-        for w, scales in enumerate((w1_scales, w2_scales)):
+        def load_scales(w, scales, queue):
             rows = scales.rearrange("z (q r) c -> r q z c", r=4)
             for r in range(4):
-                nc.gpsimd.dma_start(out=w_scales[r:P:32, w, :, :].bitcast(I32), in_=rows[r].bitcast(I32))
+                queue.dma_start(out=w_scales[w][r:P:32, :, :].bitcast(I32), in_=rows[r].bitcast(I32))
 
+        load_scales(LAYER, w1_scales, nc.gpsimd)
         raw = {}
 
-        def load_x(z, u, h):
-            raw[z, u, h] = keep.tile([P, 2, HALF], F32, name="raw_%d_%d_%d" % (z, u, h))
+        def load_rows(z, u, first, count):
             rows = xT[512 * z : 512 * (z + 1), :].rearrange("(p j) c -> p j c", j=4)
-            nc.sync.dma_start(out=raw[z, u, h][:], in_=rows[:, 2 * u : 2 * u + 2, h * HALF : (h + 1) * HALF])
+            raw[z, u, first] = keep.tile([P, 2, count], F32, name="raw_%d_%d_%d" % (z, u, first), align_bytes=64)
+            nc.sync.dma_start(out=raw[z, u, first][:], in_=rows[:, 2 * u : 2 * u + 2, first : first + count])
 
-        load_x(0, 0, 0)
+        load_rows(0, 0, 0, T)
         nc.sync.dma_start(offsets[:], offs)
-        load_x(0, 0, 1)
+        for z, u in ((0, 1), (1, 0), (1, 1)):
+            load_rows(z, u, 0, HALF)
+            load_rows(z, u, HALF, HALF)
         res_sb = keep.tile([P, T], F32, name="res_sb")
         nc.sync.dma_start(out=res_sb[:], in_=res)
-        for z, u in ((0, 1), (1, 0), (1, 1)):
-            for h in range(2):
-                load_x(z, u, h)
-        w_words = []
-        for w, words in enumerate((w1_words, w2_words)):
-            w_words.append(keep.tile([P, PASSES, 2 * N], U8, name="w_words%d" % w, align_bytes=64))
+        w_words = {}
+        for w, words in ((LAYER, w1_words), (GATE, w2_words)):
+            w_words[w] = keep.tile([P, PASSES, 2 * N], U8, name="w_words%d" % w, align_bytes=64)
             nc.sync.dma_start(out=w_words[w][:].bitcast(I32), in_=words.rearrange("z p b -> p z b").bitcast(I32))
+        load_scales(GATE, w2_scales, nc.sync)
 
         def cast_pair(z, u):
             window = keep.tile([P, T], U32, name="window_%d_%d" % (z, u))
             pairs = window[:].bitcast(BF16).rearrange("p (c e) -> p c e", e=2)
-            for h in range(2):
-                cut = SCALAR_COLS_LAST if (z, u, h) == (1, 1, 1) else SCALAR_COLS
-                src = raw[z, u, h][:].rearrange("p e c -> p c e")
-                nc.scalar.copy(pairs[:, h * HALF : h * HALF + cut, :], src[:, 0:cut, :])
-                nc.vector.tensor_copy(pairs[:, h * HALF + cut : (h + 1) * HALF, :], src[:, cut:HALF, :])
+            if (z, u) == (0, 0):
+                start, scalar_columns = 0, 2 * SCALAR_COLUMNS
+            else:
+                start, scalar_columns = HALF, SCALAR_COLUMNS
+                nc.scalar.copy(pairs[:, 0:HALF, :], raw[z, u, 0][:].rearrange("p e c -> p c e"))
+            shared = raw[z, u, start][:].rearrange("p e c -> p c e")
+            nc.scalar.copy(pairs[:, start : start + scalar_columns, :], shared[:, 0:scalar_columns, :])
+            nc.vector.tensor_copy(pairs[:, start + scalar_columns :, :], shared[:, scalar_columns:, :])
             return window
 
-        picked0 = keep.tile([P, 2, S], U32, name="picked0")
-        window = cast_pair(0, 0)
-        nc.vector.tensor_copy(picked0[:, 0, :], window[:].indirect(offsets[:]))
-        r_picked = keep.tile([P, S], F32, name="r_picked")
-        nc.vector.tensor_copy(r_picked[:], res_sb[:].indirect(offsets[:]))
-        window = cast_pair(0, 1)
-        nc.vector.tensor_copy(picked0[:, 1, :], window[:].indirect(offsets[:]))
-        woven0 = keep.tile([P, 4 * S], BF16, name="woven0", align_bytes=64)
-        nc.vector.tensor_copy(
-            woven0[:].bitcast(I32).rearrange("p (c u) -> p c u", u=2),
-            picked0[:].bitcast(I32).rearrange("p u c -> p c u"),
-        )
-        codes0 = keep.tile([P, S], U32, name="codes0", align_bytes=64)
-        scales0 = keep.tile([P, S], U8, name="scales0", align_bytes=64)
-        nc.vector.quantize_mx(out=codes0[:].bitcast(FP8X4), scales=scales0[:], in_=woven0[:])
+        def entries(first, count):
+            return offsets[:, first // 16 : (first + count) // 16]
 
-        picked1 = [keep.tile([P, 2, CHUNK], U32, name="picked1_%d" % c) for c in range(CHUNKS)]
+        woven0 = keep.tile([P, 4 * S], BF16, name="woven0", align_bytes=64)
+        for u in range(2):
+            window = cast_pair(0, u)
+            slots = woven0[:].bitcast(U32).rearrange("p (c u) -> p c u", u=2)
+            nc.vector.tensor_copy(slots[:, :, u], window[:].indirect(offsets[:]))
+
+        picked = [keep.tile([P, 2, CHUNK], U32, name="picked%d" % c) for c in range(CHUNKS)]
+
+        def pick_pair(window, u):
+            for c in range(CHUNKS):
+                nc.vector.tensor_copy(picked[c][:, u, :], window[:].indirect(entries(c * CHUNK, CHUNK)))
+
+        codes0, scales0 = [], []
         for u in range(2):
             window = cast_pair(1, u)
-            for c in range(CHUNKS):
-                piece = offsets[:, c * CHUNK // 16 : (c + 1) * CHUNK // 16]
-                nc.vector.tensor_copy(picked1[c][:, u, :], window[:].indirect(piece))
+            codes0.append(keep.tile([P, S // 2], U32, name="codes0_%d" % u, tag="raw_1_%d_0" % u, align_bytes=64))
+            scales0.append(keep.tile([P, S // 2], U8, name="scales0_%d" % u, align_bytes=64))
+            nc.vector.quantize_mx(
+                out=codes0[u][:].bitcast(FP8X4), scales=scales0[u][:], in_=woven0[:, 2 * S * u : 2 * S * (u + 1)]
+            )
+            pick_pair(window, u)
+
+        passing = [keep.tile([P, CHUNK], F32, name="passing0", tag="raw_1_1_%d" % HALF, align_bytes=64)]
+        nc.vector.tensor_copy(passing[0][:], res_sb[:].indirect(entries(0, CHUNK)))
 
         codes1, scales1 = [], []
         for c in range(CHUNKS):
             woven1 = keep.tile([P, 4 * CHUNK], BF16, name="woven1_%d" % c, align_bytes=64)
             nc.scalar.copy(
                 woven1[:].bitcast(U32).rearrange("p (c u) -> p c u", u=2),
-                picked1[c][:].rearrange("p u c -> p c u"),
+                picked[c][:].rearrange("p u c -> p c u"),
             )
             codes1.append(keep.tile([P, CHUNK], U32, name="codes1_%d" % c, align_bytes=64))
             scales1.append(keep.tile([P, CHUNK], U8, name="scales1_%d" % c, align_bytes=64))
             nc.vector.quantize_mx(out=codes1[c][:].bitcast(FP8X4), scales=scales1[c][:], in_=woven1[:])
 
+        passing.append(keep.tile([P, S - CHUNK], F32, name="passing1", tag="woven1_%d" % (CHUNKS - 1), align_bytes=64))
+        nc.vector.tensor_copy(passing[1][:], res_sb[:].indirect(entries(CHUNK, S - CHUNK)))
+
+        def product(w, c, z):
+            cols = slice(c % 2 * CHUNK, (c % 2 + 1) * CHUNK)
+            nc.tensor.matmul_mx(
+                out=sums[w, c][:],
+                lhsT=w_words[w][:, z, :].bitcast(FP4X4),
+                lhsT_scale=w_scales[w][:, z, :],
+                rhs=(codes0[c // 2][:, cols] if z == 0 else codes1[c][:]).bitcast(FP8X4),
+                rhs_scale=scales0[c // 2][:, cols] if z == 0 else scales1[c][:],
+                start=(z == 0),
+                stop=(z == PASSES - 1),
+            )
+
+        sums = {}
+        for w in (LAYER, GATE):
+            for c in range(CHUNKS):
+                sums[w, c] = psum.tile([N, CHUNK], F32, name="sums_%d_%d" % (w, c))
+                product(w, c, 0)
+        gate = []
         for c in range(CHUNKS):
-            cols = slice(c * CHUNK, (c + 1) * CHUNK)
-            sums = []
-            for w in (1, 0):
-                acc = psum.tile([N, CHUNK], F32, name="acc_%d_%d" % (w, c))
-                sums.append(acc)
-                for z in range(PASSES):
-                    nc.tensor.matmul_mx(
-                        out=acc[:],
-                        lhsT=w_words[w][:, z, :].bitcast(FP4X4),
-                        lhsT_scale=w_scales[:, w, z, :],
-                        rhs=(codes0[:, cols] if z == 0 else codes1[c][:]).bitcast(FP8X4),
-                        rhs_scale=scales0[:, cols] if z == 0 else scales1[c][:],
-                        start=(z == 0),
-                        stop=(z == PASSES - 1),
-                    )
-            gate = keep.tile([N, CHUNK], F32, name="gate%d" % c)
-            nc.scalar.activation(gate[:], sums[0][:], SIGMOID)
-            diff = keep.tile([N, CHUNK], F32, name="diff%d" % c)
-            nc.vector.scalar_tensor_tensor(diff[:], sums[1][:], 0.0, r_picked[:, cols], ALU.max, ALU.subtract)
-            gated = keep.tile([N, CHUNK], F32, name="gated%d" % c)
-            nc.vector.tensor_tensor(gated[:], diff[:], gate[:], ALU.mult)
-            result = keep.tile([N, CHUNK], F32, name="result%d" % c)
-            nc.vector.tensor_tensor(result[:], gated[:], r_picked[:, cols], ALU.add)
-            nc.sync.dma_start(out=out[:, cols], in_=result[:])
+            product(GATE, c, 1)
+            product(LAYER, c, 1)
+            gate.append(keep.tile([N, CHUNK], F32, name="gate%d" % c))
+            nc.scalar.activation(gate[c][:], sums[GATE, c][:], SIGMOID)
+
+        r = [passing[0][:]] + [passing[1][:, c * CHUNK : (c + 1) * CHUNK] for c in range(CHUNKS - 1)]
+        diff = [keep.tile([N, CHUNK], F32, name="diff%d" % c) for c in range(CHUNKS)]
+        gated = [keep.tile([N, CHUNK], F32, name="gated%d" % c) for c in range(CHUNKS)]
+        result = [keep.tile([N, CHUNK], F32, name="result%d" % c) for c in range(CHUNKS)]
+        for step in range(CHUNKS + 2):
+            if step < CHUNKS:
+                c = step
+                nc.vector.scalar_tensor_tensor(diff[c][:], sums[LAYER, c][:], 0.0, r[c], ALU.max, ALU.subtract)
+            if 1 <= step <= CHUNKS:
+                c = step - 1
+                nc.vector.tensor_tensor(gated[c][:], diff[c][:], gate[c][:], ALU.mult)
+            if step >= 2:
+                c = step - 2
+                nc.vector.tensor_tensor(result[c][:], gated[c][:], r[c], ALU.add)
+                nc.sync.dma_start(out=out[:, c * CHUNK : (c + 1) * CHUNK], in_=result[c][:])

@@ -17,24 +17,30 @@ ALU = mybir.AluOpType
 SIGMOID = mybir.ActivationFunctionType.Sigmoid
 
 P = 128
-PASSES = K // 512
-HALF = T // 2
+K_PASS = 4 * P
+PASSES = K // K_PASS
+HALF_T = T // 2
+HALF_S = S // 2
 CHUNK = 128
 CHUNKS = S // CHUNK
-SCALAR_COLUMNS = 176
+SCALAR_SHARE = 176
 LAYER, GATE = 0, 1
 
 
-def tile_picked_highway_relu_l_kernel(tc, xT, res, w1_words, w1_scales, w2_words, w2_scales, offs, out):
+def tile_picked_highway_relu_l_kernel(
+    tc, xT, res, w1_words, w1_scales, w2_words, w2_scales, offs, out
+):
     nc = tc.nc
     with ExitStack() as ctx:
         keep = ctx.enter_context(tc.tile_pool(name="keep", bufs=1))
         psum = ctx.enter_context(tc.psum_pool(name="psum", bufs=1))
 
         offsets = keep.tile([P, S // 16], U16, name="offsets")
+
         w_scales = [keep.tile([P, PASSES, N], U8, name="w_scales%d" % w, align_bytes=64) for w in (LAYER, GATE)]
         for w in (LAYER, GATE):
             nc.gpsimd.memset(w_scales[w][:].rearrange("p z c -> p (z c)").bitcast(I32), 0)
+
         warm = keep.tile([P, 8], F32, name="warm")
         warm_out = keep.tile([P, 8], F32, name="warm_out")
         nc.vector.memset(warm[:], 0.0)
@@ -45,19 +51,22 @@ def tile_picked_highway_relu_l_kernel(tc, xT, res, w1_words, w1_scales, w2_words
             for r in range(4):
                 queue.dma_start(out=w_scales[w][r:P:32, :, :].bitcast(I32), in_=rows[r].bitcast(I32))
 
-        load_scales(LAYER, w1_scales, nc.gpsimd)
         raw = {}
 
-        def load_rows(z, u, first, count):
-            rows = xT[512 * z : 512 * (z + 1), :].rearrange("(p j) c -> p j c", j=4)
-            raw[z, u, first] = keep.tile([P, 2, count], F32, name="raw_%d_%d_%d" % (z, u, first), align_bytes=64)
+        def raw_tag(z, u, first):
+            return "raw_%d_%d_%d" % (z, u, first)
+
+        def load_pair(z, u, first, count):
+            rows = xT[K_PASS * z : K_PASS * (z + 1), :].rearrange("(p t) c -> p t c", t=4)
+            raw[z, u, first] = keep.tile([P, 2, count], F32, name=raw_tag(z, u, first), align_bytes=64)
             nc.sync.dma_start(out=raw[z, u, first][:], in_=rows[:, 2 * u : 2 * u + 2, first : first + count])
 
-        load_rows(0, 0, 0, T)
+        load_scales(LAYER, w1_scales, nc.gpsimd)
+        load_pair(0, 0, 0, T)
         nc.sync.dma_start(offsets[:], offs)
         for z, u in ((0, 1), (1, 0), (1, 1)):
-            load_rows(z, u, 0, HALF)
-            load_rows(z, u, HALF, HALF)
+            load_pair(z, u, 0, HALF_T)
+            load_pair(z, u, HALF_T, HALF_T)
         res_sb = keep.tile([P, T], F32, name="res_sb")
         nc.sync.dma_start(out=res_sb[:], in_=res)
         w_words = {}
@@ -68,72 +77,86 @@ def tile_picked_highway_relu_l_kernel(tc, xT, res, w1_words, w1_scales, w2_words
 
         def cast_pair(z, u):
             window = keep.tile([P, T], U32, name="window_%d_%d" % (z, u))
-            pairs = window[:].bitcast(BF16).rearrange("p (c e) -> p c e", e=2)
-            if (z, u) == (0, 0):
-                start, scalar_columns = 0, 2 * SCALAR_COLUMNS
+            values = window[:].bitcast(BF16).rearrange("p (c e) -> p c e", e=2)
+            if (z, u, HALF_T) in raw:
+                first, share = HALF_T, SCALAR_SHARE
+                nc.scalar.copy(values[:, 0:HALF_T, :], raw[z, u, 0][:].rearrange("p e c -> p c e"))
             else:
-                start, scalar_columns = HALF, SCALAR_COLUMNS
-                nc.scalar.copy(pairs[:, 0:HALF, :], raw[z, u, 0][:].rearrange("p e c -> p c e"))
-            shared = raw[z, u, start][:].rearrange("p e c -> p c e")
-            nc.scalar.copy(pairs[:, start : start + scalar_columns, :], shared[:, 0:scalar_columns, :])
-            nc.vector.tensor_copy(pairs[:, start + scalar_columns :, :], shared[:, scalar_columns:, :])
+                first, share = 0, 2 * SCALAR_SHARE
+            shared = raw[z, u, first][:].rearrange("p e c -> p c e")
+            nc.scalar.copy(values[:, first : first + share, :], shared[:, 0:share, :])
+            nc.vector.tensor_copy(values[:, first + share :, :], shared[:, share:, :])
             return window
 
         def entries(first, count):
             return offsets[:, first // 16 : (first + count) // 16]
 
-        woven0 = keep.tile([P, 4 * S], BF16, name="woven0", align_bytes=64)
+        def gather_pair(window, u, picked):
+            count = S // len(picked)
+            for i, tile in enumerate(picked):
+                nc.vector.tensor_copy(tile[:, u, :], window[:].indirect(entries(i * count, count)))
+
+        def weave(copy, word_dtype, woven, picked):
+            copy(
+                woven[:].bitcast(word_dtype).rearrange("p (c u) -> p c u", u=2),
+                picked[:].bitcast(word_dtype).rearrange("p u c -> p c u"),
+            )
+
+        picked0 = [keep.tile([P, 2, HALF_S], U32, name="picked0_%d" % h) for h in range(2)]
         for u in range(2):
-            window = cast_pair(0, u)
-            slots = woven0[:].bitcast(U32).rearrange("p (c u) -> p c u", u=2)
-            nc.vector.tensor_copy(slots[:, :, u], window[:].indirect(offsets[:]))
+            gather_pair(cast_pair(0, u), u, picked0)
+        woven0 = [keep.tile([P, 4 * HALF_S], BF16, name="woven0_0", align_bytes=64)]
+        weave(nc.vector.tensor_copy, I32, woven0[0], picked0[0])
 
-        picked = [keep.tile([P, 2, CHUNK], U32, name="picked%d" % c) for c in range(CHUNKS)]
-
-        def pick_pair(window, u):
-            for c in range(CHUNKS):
-                nc.vector.tensor_copy(picked[c][:, u, :], window[:].indirect(entries(c * CHUNK, CHUNK)))
-
+        picked1 = [keep.tile([P, 2, CHUNK], U32, name="picked1_%d" % c) for c in range(CHUNKS)]
         codes0, scales0 = [], []
         for u in range(2):
             window = cast_pair(1, u)
-            codes0.append(keep.tile([P, S // 2], U32, name="codes0_%d" % u, tag="raw_1_%d_0" % u, align_bytes=64))
-            scales0.append(keep.tile([P, S // 2], U8, name="scales0_%d" % u, align_bytes=64))
-            nc.vector.quantize_mx(
-                out=codes0[u][:].bitcast(FP8X4), scales=scales0[u][:], in_=woven0[:, 2 * S * u : 2 * S * (u + 1)]
-            )
-            pick_pair(window, u)
+            codes0.append(keep.tile([P, HALF_S], U32, name="codes0_%d" % u, tag=raw_tag(1, u, 0), align_bytes=64))
+            scales0.append(keep.tile([P, HALF_S], U8, name="scales0_%d" % u, align_bytes=64))
+            nc.vector.quantize_mx(out=codes0[u][:].bitcast(FP8X4), scales=scales0[u][:], in_=woven0[u][:])
+            gather_pair(window, u, picked1)
+            if u == 0:
+                woven0.append(
+                    keep.tile([P, 4 * HALF_S], BF16, name="woven0_1", tag=raw_tag(1, 0, HALF_T), align_bytes=64)
+                )
+                weave(nc.scalar.copy, U32, woven0[1], picked0[1])
 
-        passing = [keep.tile([P, CHUNK], F32, name="passing0", tag="raw_1_1_%d" % HALF, align_bytes=64)]
-        nc.vector.tensor_copy(passing[0][:], res_sb[:].indirect(entries(0, CHUNK)))
+        passing_first = keep.tile([P, CHUNK], F32, name="passing_first", tag=raw_tag(1, 1, HALF_T), align_bytes=64)
+        nc.vector.tensor_copy(passing_first[:], res_sb[:].indirect(entries(0, CHUNK)))
 
         codes1, scales1 = [], []
         for c in range(CHUNKS):
             woven1 = keep.tile([P, 4 * CHUNK], BF16, name="woven1_%d" % c, align_bytes=64)
-            nc.scalar.copy(
-                woven1[:].bitcast(U32).rearrange("p (c u) -> p c u", u=2),
-                picked[c][:].rearrange("p u c -> p c u"),
-            )
+            weave(nc.scalar.copy, U32, woven1, picked1[c])
             codes1.append(keep.tile([P, CHUNK], U32, name="codes1_%d" % c, align_bytes=64))
             scales1.append(keep.tile([P, CHUNK], U8, name="scales1_%d" % c, align_bytes=64))
             nc.vector.quantize_mx(out=codes1[c][:].bitcast(FP8X4), scales=scales1[c][:], in_=woven1[:])
 
-        passing.append(keep.tile([P, S - CHUNK], F32, name="passing1", tag="woven1_%d" % (CHUNKS - 1), align_bytes=64))
-        nc.vector.tensor_copy(passing[1][:], res_sb[:].indirect(entries(CHUNK, S - CHUNK)))
+        passing_rest = keep.tile(
+            [P, S - CHUNK], F32, name="passing_rest", tag="woven1_%d" % (CHUNKS - 1), align_bytes=64
+        )
+        nc.vector.tensor_copy(passing_rest[:], res_sb[:].indirect(entries(CHUNK, S - CHUNK)))
+        passing = [passing_first[:]] + [passing_rest[:, c * CHUNK : (c + 1) * CHUNK] for c in range(CHUNKS - 1)]
+
+        sums = {}
 
         def product(w, c, z):
-            cols = slice(c % 2 * CHUNK, (c % 2 + 1) * CHUNK)
+            if z == 0:
+                half, first = divmod(c * CHUNK, HALF_S)
+                codes, scales = codes0[half][:, first : first + CHUNK], scales0[half][:, first : first + CHUNK]
+            else:
+                codes, scales = codes1[c][:], scales1[c][:]
             nc.tensor.matmul_mx(
                 out=sums[w, c][:],
                 lhsT=w_words[w][:, z, :].bitcast(FP4X4),
                 lhsT_scale=w_scales[w][:, z, :],
-                rhs=(codes0[c // 2][:, cols] if z == 0 else codes1[c][:]).bitcast(FP8X4),
-                rhs_scale=scales0[c // 2][:, cols] if z == 0 else scales1[c][:],
+                rhs=codes.bitcast(FP8X4),
+                rhs_scale=scales,
                 start=(z == 0),
                 stop=(z == PASSES - 1),
             )
 
-        sums = {}
         for w in (LAYER, GATE):
             for c in range(CHUNKS):
                 sums[w, c] = psum.tile([N, CHUNK], F32, name="sums_%d_%d" % (w, c))
@@ -145,18 +168,17 @@ def tile_picked_highway_relu_l_kernel(tc, xT, res, w1_words, w1_scales, w2_words
             gate.append(keep.tile([N, CHUNK], F32, name="gate%d" % c))
             nc.scalar.activation(gate[c][:], sums[GATE, c][:], SIGMOID)
 
-        r = [passing[0][:]] + [passing[1][:, c * CHUNK : (c + 1) * CHUNK] for c in range(CHUNKS - 1)]
         diff = [keep.tile([N, CHUNK], F32, name="diff%d" % c) for c in range(CHUNKS)]
         gated = [keep.tile([N, CHUNK], F32, name="gated%d" % c) for c in range(CHUNKS)]
         result = [keep.tile([N, CHUNK], F32, name="result%d" % c) for c in range(CHUNKS)]
         for step in range(CHUNKS + 2):
             if step < CHUNKS:
                 c = step
-                nc.vector.scalar_tensor_tensor(diff[c][:], sums[LAYER, c][:], 0.0, r[c], ALU.max, ALU.subtract)
+                nc.vector.scalar_tensor_tensor(diff[c][:], sums[LAYER, c][:], 0.0, passing[c], ALU.max, ALU.subtract)
             if 1 <= step <= CHUNKS:
                 c = step - 1
                 nc.vector.tensor_tensor(gated[c][:], diff[c][:], gate[c][:], ALU.mult)
             if step >= 2:
                 c = step - 2
-                nc.vector.tensor_tensor(result[c][:], gated[c][:], r[c], ALU.add)
+                nc.vector.tensor_tensor(result[c][:], gated[c][:], passing[c], ALU.add)
                 nc.sync.dma_start(out=out[:, c * CHUNK : (c + 1) * CHUNK], in_=result[c][:])

@@ -24,6 +24,7 @@ HALF_S = S // 2
 CHUNK = 128
 CHUNKS = S // CHUNK
 SCALAR_SHARE = 176
+EARLY = 1
 LAYER, GATE = 0, 1
 
 
@@ -67,13 +68,17 @@ def tile_picked_highway_relu_l_kernel(
         for z, u in ((0, 1), (1, 0), (1, 1)):
             load_pair(z, u, 0, HALF_T)
             load_pair(z, u, HALF_T, HALF_T)
-        res_sb = keep.tile([P, T], F32, name="res_sb")
-        nc.sync.dma_start(out=res_sb[:], in_=res)
         w_words = {}
-        for w, words in ((LAYER, w1_words), (GATE, w2_words)):
+
+        def load_words(w, words):
             w_words[w] = keep.tile([P, PASSES, 2 * N], U8, name="w_words%d" % w, align_bytes=64)
             nc.sync.dma_start(out=w_words[w][:].bitcast(I32), in_=words.rearrange("z p b -> p z b").bitcast(I32))
+
+        load_words(LAYER, w1_words)
+        load_words(GATE, w2_words)
         load_scales(GATE, w2_scales, nc.sync)
+        res_sb = keep.tile([P, T], F32, name="res_sb")
+        nc.sync.dma_start(out=res_sb[:], in_=res)
 
         def cast_pair(z, u):
             window = keep.tile([P, T], U32, name="window_%d_%d" % (z, u))
@@ -99,45 +104,39 @@ def tile_picked_highway_relu_l_kernel(
         def weave(copy, word_dtype, woven, picked):
             copy(
                 woven[:].bitcast(word_dtype).rearrange("p (c u) -> p c u", u=2),
-                picked[:].bitcast(word_dtype).rearrange("p u c -> p c u"),
+                picked.bitcast(word_dtype).rearrange("p u c -> p c u"),
             )
 
         picked0 = [keep.tile([P, 2, HALF_S], U32, name="picked0_%d" % h) for h in range(2)]
         for u in range(2):
             gather_pair(cast_pair(0, u), u, picked0)
         woven0 = [keep.tile([P, 4 * HALF_S], BF16, name="woven0_0", align_bytes=64)]
-        weave(nc.vector.tensor_copy, I32, woven0[0], picked0[0])
+        weave(nc.vector.tensor_copy, I32, woven0[0], picked0[0][:])
 
-        picked1 = [keep.tile([P, 2, CHUNK], U32, name="picked1_%d" % c) for c in range(CHUNKS)]
+        picked1 = keep.tile([P, 2, S], U32, name="picked1")
         codes0, scales0 = [], []
         for u in range(2):
             window = cast_pair(1, u)
             codes0.append(keep.tile([P, HALF_S], U32, name="codes0_%d" % u, tag=raw_tag(1, u, 0), align_bytes=64))
             scales0.append(keep.tile([P, HALF_S], U8, name="scales0_%d" % u, align_bytes=64))
             nc.vector.quantize_mx(out=codes0[u][:].bitcast(FP8X4), scales=scales0[u][:], in_=woven0[u][:])
-            gather_pair(window, u, picked1)
+            count = S if u == 0 else CHUNK
+            for first in range(0, S, count):
+                nc.vector.tensor_copy(picked1[:, u, first : first + count], window[:].indirect(entries(first, count)))
             if u == 0:
                 woven0.append(
                     keep.tile([P, 4 * HALF_S], BF16, name="woven0_1", tag=raw_tag(1, 0, HALF_T), align_bytes=64)
                 )
-                weave(nc.scalar.copy, U32, woven0[1], picked0[1])
+                weave(nc.scalar.copy, U32, woven0[1], picked0[1][:])
 
-        passing_first = keep.tile([P, CHUNK], F32, name="passing_first", tag=raw_tag(1, 1, HALF_T), align_bytes=64)
-        nc.vector.tensor_copy(passing_first[:], res_sb[:].indirect(entries(0, CHUNK)))
-
+        codes1_all = keep.tile([P, S], U32, name="codes1", tag=raw_tag(1, 0, 0), align_bytes=64)
         codes1, scales1 = [], []
         for c in range(CHUNKS):
             woven1 = keep.tile([P, 4 * CHUNK], BF16, name="woven1_%d" % c, align_bytes=64)
-            weave(nc.scalar.copy, U32, woven1, picked1[c])
-            codes1.append(keep.tile([P, CHUNK], U32, name="codes1_%d" % c, align_bytes=64))
+            weave(nc.scalar.copy, U32, woven1, picked1[:, :, c * CHUNK : (c + 1) * CHUNK])
+            codes1.append(codes1_all[:, c * CHUNK : (c + 1) * CHUNK])
             scales1.append(keep.tile([P, CHUNK], U8, name="scales1_%d" % c, align_bytes=64))
-            nc.vector.quantize_mx(out=codes1[c][:].bitcast(FP8X4), scales=scales1[c][:], in_=woven1[:])
-
-        passing_rest = keep.tile(
-            [P, S - CHUNK], F32, name="passing_rest", tag="woven1_%d" % (CHUNKS - 1), align_bytes=64
-        )
-        nc.vector.tensor_copy(passing_rest[:], res_sb[:].indirect(entries(CHUNK, S - CHUNK)))
-        passing = [passing_first[:]] + [passing_rest[:, c * CHUNK : (c + 1) * CHUNK] for c in range(CHUNKS - 1)]
+            nc.vector.quantize_mx(out=codes1[c].bitcast(FP8X4), scales=scales1[c][:], in_=woven1[:])
 
         sums = {}
 
@@ -146,7 +145,7 @@ def tile_picked_highway_relu_l_kernel(
                 half, first = divmod(c * CHUNK, HALF_S)
                 codes, scales = codes0[half][:, first : first + CHUNK], scales0[half][:, first : first + CHUNK]
             else:
-                codes, scales = codes1[c][:], scales1[c][:]
+                codes, scales = codes1[c], scales1[c][:]
             nc.tensor.matmul_mx(
                 out=sums[w, c][:],
                 lhsT=w_words[w][:, z, :].bitcast(FP4X4),
@@ -161,24 +160,37 @@ def tile_picked_highway_relu_l_kernel(
             for c in range(CHUNKS):
                 sums[w, c] = psum.tile([N, CHUNK], F32, name="sums_%d_%d" % (w, c))
                 product(w, c, 0)
-        gate = []
-        for c in range(CHUNKS):
-            product(GATE, c, 1)
-            product(LAYER, c, 1)
-            gate.append(keep.tile([N, CHUNK], F32, name="gate%d" % c))
-            nc.scalar.activation(gate[c][:], sums[GATE, c][:], SIGMOID)
+        for w in (GATE, LAYER):
+            for c in range(CHUNKS):
+                product(w, c, 1)
 
-        diff = [keep.tile([N, CHUNK], F32, name="diff%d" % c) for c in range(CHUNKS)]
-        gated = [keep.tile([N, CHUNK], F32, name="gated%d" % c) for c in range(CHUNKS)]
+        early = keep.tile([P, EARLY * CHUNK], F32, name="early", tag="woven1_%d" % (CHUNKS - 2), align_bytes=64)
+        nc.vector.tensor_copy(early[:], res_sb[:].indirect(entries(0, EARLY * CHUNK)))
+
+        gate = [keep.tile([N, CHUNK], F32, name="gate%d" % c) for c in range(CHUNKS)]
+        rest = [keep.tile([N, CHUNK], F32, name="rest%d" % c) for c in range(CHUNKS)]
+        for step in range(CHUNKS + 1):
+            if step < CHUNKS:
+                nc.scalar.activation(rest[step][:], sums[GATE, step][:], SIGMOID, scale=-1.0)
+            if step >= 1:
+                nc.scalar.activation(gate[step - 1][:], sums[GATE, step - 1][:], SIGMOID)
+
+        kept = [keep.tile([N, CHUNK], F32, name="kept%d" % c) for c in range(CHUNKS)]
+        gated_all = keep.tile([N, S], F32, name="gated_all", tag="woven1_%d" % (CHUNKS - 2), align_bytes=64)
+        gated = [gated_all[:, c * CHUNK : (c + 1) * CHUNK] for c in range(CHUNKS)]
         result = [keep.tile([N, CHUNK], F32, name="result%d" % c) for c in range(CHUNKS)]
         for step in range(CHUNKS + 2):
             if step < CHUNKS:
                 c = step
-                nc.vector.scalar_tensor_tensor(diff[c][:], sums[LAYER, c][:], 0.0, passing[c], ALU.max, ALU.subtract)
+                if c < EARLY:
+                    passing = early[:, c * CHUNK : (c + 1) * CHUNK]
+                else:
+                    passing = res_sb[:].indirect(entries(c * CHUNK, CHUNK))
+                nc.vector.tensor_tensor(kept[c][:], passing, rest[c][:], ALU.mult)
             if 1 <= step <= CHUNKS:
                 c = step - 1
-                nc.vector.tensor_tensor(gated[c][:], diff[c][:], gate[c][:], ALU.mult)
+                nc.vector.scalar_tensor_tensor(gated[c], sums[LAYER, c][:], 0.0, gate[c][:], ALU.max, ALU.mult)
             if step >= 2:
                 c = step - 2
-                nc.vector.tensor_tensor(result[c][:], gated[c][:], passing[c], ALU.add)
+                nc.vector.tensor_tensor(result[c][:], gated[c], kept[c][:], ALU.add)
                 nc.sync.dma_start(out=out[:, c * CHUNK : (c + 1) * CHUNK], in_=result[c][:])

@@ -24,7 +24,6 @@ HALF_S = S // 2
 CHUNK = 128
 CHUNKS = S // CHUNK
 SCALAR_SHARE = 176
-EARLY = 1
 LAYER, GATE = 0, 1
 
 
@@ -68,17 +67,20 @@ def tile_picked_highway_relu_l_kernel(
         for z, u in ((0, 1), (1, 0), (1, 1)):
             load_pair(z, u, 0, HALF_T)
             load_pair(z, u, HALF_T, HALF_T)
-        w_words = {}
-
-        def load_words(w, words):
-            w_words[w] = keep.tile([P, PASSES, 2 * N], U8, name="w_words%d" % w, align_bytes=64)
-            nc.sync.dma_start(out=w_words[w][:].bitcast(I32), in_=words.rearrange("z p b -> p z b").bitcast(I32))
-
-        load_words(LAYER, w1_words)
-        load_words(GATE, w2_words)
-        load_scales(GATE, w2_scales, nc.sync)
         res_sb = keep.tile([P, T], F32, name="res_sb")
         nc.sync.dma_start(out=res_sb[:], in_=res)
+        w_words = [keep.tile([P, PASSES, 2 * N], U8, name="w_words%d" % w, align_bytes=64) for w in (LAYER, GATE)]
+
+        def load_words(w, words, passes):
+            nc.sync.dma_start(
+                out=w_words[w][:, passes, :].bitcast(I32),
+                in_=words.rearrange("z p b -> p z b")[:, passes, :].bitcast(I32),
+            )
+
+        load_words(LAYER, w1_words, slice(0, 1))
+        load_words(GATE, w2_words, slice(0, PASSES))
+        load_scales(GATE, w2_scales, nc.sync)
+        load_words(LAYER, w1_words, slice(1, PASSES))
 
         def cast_pair(z, u):
             window = keep.tile([P, T], U32, name="window_%d_%d" % (z, u))
@@ -96,10 +98,9 @@ def tile_picked_highway_relu_l_kernel(
         def entries(first, count):
             return offsets[:, first // 16 : (first + count) // 16]
 
-        def gather_pair(window, u, picked):
-            count = S // len(picked)
-            for i, tile in enumerate(picked):
-                nc.vector.tensor_copy(tile[:, u, :], window[:].indirect(entries(i * count, count)))
+        def gather_pair(window, picked, count):
+            for first in range(0, S, count):
+                nc.vector.tensor_copy(picked[:, first : first + count], window[:].indirect(entries(first, count)))
 
         def weave(copy, word_dtype, woven, picked):
             copy(
@@ -107,11 +108,11 @@ def tile_picked_highway_relu_l_kernel(
                 picked.bitcast(word_dtype).rearrange("p u c -> p c u"),
             )
 
-        picked0 = [keep.tile([P, 2, HALF_S], U32, name="picked0_%d" % h) for h in range(2)]
+        picked0 = keep.tile([P, 2, S], U32, name="picked0")
         for u in range(2):
-            gather_pair(cast_pair(0, u), u, picked0)
+            gather_pair(cast_pair(0, u), picked0[:, u, :], S if u == 0 else HALF_S)
         woven0 = [keep.tile([P, 4 * HALF_S], BF16, name="woven0_0", align_bytes=64)]
-        weave(nc.vector.tensor_copy, I32, woven0[0], picked0[0][:])
+        weave(nc.vector.tensor_copy, I32, woven0[0], picked0[:, :, 0:HALF_S])
 
         picked1 = keep.tile([P, 2, S], U32, name="picked1")
         codes0, scales0 = [], []
@@ -120,16 +121,16 @@ def tile_picked_highway_relu_l_kernel(
             codes0.append(keep.tile([P, HALF_S], U32, name="codes0_%d" % u, tag=raw_tag(1, u, 0), align_bytes=64))
             scales0.append(keep.tile([P, HALF_S], U8, name="scales0_%d" % u, align_bytes=64))
             nc.vector.quantize_mx(out=codes0[u][:].bitcast(FP8X4), scales=scales0[u][:], in_=woven0[u][:])
-            count = S if u == 0 else CHUNK
-            for first in range(0, S, count):
-                nc.vector.tensor_copy(picked1[:, u, first : first + count], window[:].indirect(entries(first, count)))
+            gather_pair(window, picked1[:, u, :], S if u == 0 else CHUNK)
             if u == 0:
                 woven0.append(
                     keep.tile([P, 4 * HALF_S], BF16, name="woven0_1", tag=raw_tag(1, 0, HALF_T), align_bytes=64)
                 )
-                weave(nc.scalar.copy, U32, woven0[1], picked0[1][:])
+                weave(nc.scalar.copy, U32, woven0[1], picked0[:, :, HALF_S:S])
 
-        codes1_all = keep.tile([P, S], U32, name="codes1", tag=raw_tag(1, 0, 0), align_bytes=64)
+        passing_first = keep.tile([P, CHUNK], F32, name="passing_first", tag=raw_tag(1, 1, HALF_T), align_bytes=64)
+        nc.vector.tensor_copy(passing_first[:], res_sb[:].indirect(entries(0, CHUNK)))
+        codes1_all = keep.tile([P, S], U32, name="codes1", align_bytes=64)
         codes1, scales1 = [], []
         for c in range(CHUNKS):
             woven1 = keep.tile([P, 4 * CHUNK], BF16, name="woven1_%d" % c, align_bytes=64)
@@ -160,37 +161,42 @@ def tile_picked_highway_relu_l_kernel(
             for c in range(CHUNKS):
                 sums[w, c] = psum.tile([N, CHUNK], F32, name="sums_%d_%d" % (w, c))
                 product(w, c, 0)
-        for w in (GATE, LAYER):
-            for c in range(CHUNKS):
-                product(w, c, 1)
+        gate = keep.tile([N, S], F32, name="gate")
 
-        early = keep.tile([P, EARLY * CHUNK], F32, name="early", tag="woven1_%d" % (CHUNKS - 2), align_bytes=64)
-        nc.vector.tensor_copy(early[:], res_sb[:].indirect(entries(0, EARLY * CHUNK)))
+        def columns(c, chunks=1):
+            return slice(c * CHUNK, (c + chunks) * CHUNK)
 
-        gate = [keep.tile([N, CHUNK], F32, name="gate%d" % c) for c in range(CHUNKS)]
-        rest = [keep.tile([N, CHUNK], F32, name="rest%d" % c) for c in range(CHUNKS)]
-        for step in range(CHUNKS + 1):
-            if step < CHUNKS:
-                nc.scalar.activation(rest[step][:], sums[GATE, step][:], SIGMOID, scale=-1.0)
-            if step >= 1:
-                nc.scalar.activation(gate[step - 1][:], sums[GATE, step - 1][:], SIGMOID)
+        for c in range(CHUNKS):
+            product(LAYER, c, 1)
+            product(GATE, c, 1)
+            nc.scalar.activation(gate[:, columns(c)], sums[GATE, c][:], SIGMOID)
 
-        kept = [keep.tile([N, CHUNK], F32, name="kept%d" % c) for c in range(CHUNKS)]
-        gated_all = keep.tile([N, S], F32, name="gated_all", tag="woven1_%d" % (CHUNKS - 2), align_bytes=64)
-        gated = [gated_all[:, c * CHUNK : (c + 1) * CHUNK] for c in range(CHUNKS)]
-        result = [keep.tile([N, CHUNK], F32, name="result%d" % c) for c in range(CHUNKS)]
-        for step in range(CHUNKS + 2):
-            if step < CHUNKS:
-                c = step
-                if c < EARLY:
-                    passing = early[:, c * CHUNK : (c + 1) * CHUNK]
-                else:
-                    passing = res_sb[:].indirect(entries(c * CHUNK, CHUNK))
-                nc.vector.tensor_tensor(kept[c][:], passing, rest[c][:], ALU.mult)
-            if 1 <= step <= CHUNKS:
-                c = step - 1
-                nc.vector.scalar_tensor_tensor(gated[c], sums[LAYER, c][:], 0.0, gate[c][:], ALU.max, ALU.mult)
-            if step >= 2:
-                c = step - 2
-                nc.vector.tensor_tensor(result[c][:], gated[c], kept[c][:], ALU.add)
-                nc.sync.dma_start(out=out[:, c * CHUNK : (c + 1) * CHUNK], in_=result[c][:])
+        passing_rest = keep.tile(
+            [P, S - CHUNK], F32, name="passing_rest", tag="woven1_%d" % (CHUNKS - 2), align_bytes=64
+        )
+        nc.vector.tensor_copy(passing_rest[:], res_sb[:].indirect(entries(CHUNK, S - CHUNK)))
+        passing = [passing_first[:]] + [passing_rest[:, columns(c)] for c in range(CHUNKS - 1)]
+        diff = keep.tile([N, S], F32, name="diff")
+        gated = keep.tile([N, S], F32, name="gated")
+        result = keep.tile([N, S], F32, name="result")
+
+        def subtract(c):
+            nc.vector.scalar_tensor_tensor(diff[:, columns(c)], sums[LAYER, c][:], 0.0, passing[c], ALU.max, ALU.subtract)
+
+        def multiply(cols):
+            nc.vector.tensor_tensor(gated[:, cols], diff[:, cols], gate[:, cols], ALU.mult)
+
+        def finish(c):
+            nc.vector.tensor_tensor(result[:, columns(c)], gated[:, columns(c)], passing[c], ALU.add)
+            nc.sync.dma_start(out=out[:, columns(c)], in_=result[:, columns(c)])
+
+        subtract(0)
+        subtract(1)
+        subtract(2)
+        multiply(columns(0, 2))
+        subtract(3)
+        finish(0)
+        finish(1)
+        multiply(columns(2, 2))
+        finish(2)
+        finish(3)

@@ -62,6 +62,7 @@ def tile_picked_highway_relu_l_kernel(
             nc.sync.dma_start(out=raw[z, u, first][:], in_=rows[:, 2 * u : 2 * u + 2, first : first + count])
 
         load_scales(LAYER, w1_scales, nc.gpsimd)
+        load_scales(GATE, w2_scales, nc.gpsimd)
         load_pair(0, 0, 0, T)
         nc.sync.dma_start(offsets[:], offs)
         for z, u in ((0, 1), (1, 0), (1, 1)):
@@ -79,7 +80,6 @@ def tile_picked_highway_relu_l_kernel(
 
         load_words(LAYER, w1_words, slice(0, 1))
         load_words(GATE, w2_words, slice(0, PASSES))
-        load_scales(GATE, w2_scales, nc.sync)
         load_words(LAYER, w1_words, slice(1, PASSES))
 
         def cast_pair(z, u):

@@ -68,8 +68,6 @@ def tile_picked_highway_relu_l_kernel(
         for z, u in ((0, 1), (1, 0), (1, 1)):
             load_pair(z, u, 0, HALF_T)
             load_pair(z, u, HALF_T, HALF_T)
-        res_sb = keep.tile([P, T], F32, name="res_sb")
-        nc.sync.dma_start(out=res_sb[:], in_=res)
         w_words = [keep.tile([P, PASSES, 2 * N], U8, name="w_words%d" % w, align_bytes=64) for w in (LAYER, GATE)]
 
         def load_words(w, words, passes):
@@ -79,6 +77,8 @@ def tile_picked_highway_relu_l_kernel(
             )
 
         load_words(LAYER, w1_words, slice(0, 1))
+        res_sb = keep.tile([P, T], F32, name="res_sb")
+        nc.sync.dma_start(out=res_sb[:], in_=res)
         load_words(GATE, w2_words, slice(0, PASSES))
         load_words(LAYER, w1_words, slice(1, PASSES))
 
@@ -193,10 +193,10 @@ def tile_picked_highway_relu_l_kernel(
         subtract(0)
         subtract(1)
         subtract(2)
-        multiply(columns(0, 2))
         subtract(3)
+        for c in range(CHUNKS):
+            multiply(columns(c))
         finish(0)
         finish(1)
-        multiply(columns(2, 2))
         finish(2)
         finish(3)

@@ -114,7 +114,7 @@ def tile_picked_highway_relu_l_kernel(
         woven0 = [keep.tile([P, 4 * HALF_S], BF16, name="woven0_0", align_bytes=64)]
         weave(nc.vector.tensor_copy, I32, woven0[0], picked0[:, :, 0:HALF_S])
 
-        picked1 = keep.tile([P, 2, S], U32, name="picked1")
+        picked1 = keep.tile([P, 2, S], U32, name="picked1", align_bytes=64)
         codes0, scales0 = [], []
         for u in range(2):
             window = cast_pair(1, u)
@@ -128,8 +128,8 @@ def tile_picked_highway_relu_l_kernel(
                 )
                 weave(nc.scalar.copy, U32, woven0[1], picked0[:, :, HALF_S:S])
 
-        passing_first = keep.tile([P, CHUNK], F32, name="passing_first", tag=raw_tag(1, 1, HALF_T), align_bytes=64)
-        nc.vector.tensor_copy(passing_first[:], res_sb[:].indirect(entries(0, CHUNK)))
+        passing_first = keep.tile([P, HALF_S], F32, name="passing_first", tag=raw_tag(1, 1, HALF_T), align_bytes=64)
+        nc.vector.tensor_copy(passing_first[:], res_sb[:].indirect(entries(0, HALF_S)))
         codes1_all = keep.tile([P, S], U32, name="codes1", align_bytes=64)
         codes1, scales1 = [], []
         for c in range(CHUNKS):
@@ -172,10 +172,10 @@ def tile_picked_highway_relu_l_kernel(
             nc.scalar.activation(gate[:, columns(c)], sums[GATE, c][:], SIGMOID)
 
         passing_rest = keep.tile(
-            [P, S - CHUNK], F32, name="passing_rest", tag="woven1_%d" % (CHUNKS - 2), align_bytes=64
+            [P, HALF_S], F32, name="passing_rest", tag="picked1", align_bytes=64
         )
-        nc.vector.tensor_copy(passing_rest[:], res_sb[:].indirect(entries(CHUNK, S - CHUNK)))
-        passing = [passing_first[:]] + [passing_rest[:, columns(c)] for c in range(CHUNKS - 1)]
+        nc.vector.tensor_copy(passing_rest[:], res_sb[:].indirect(entries(HALF_S, HALF_S)))
+        passing = [tile[:, columns(c)] for tile in (passing_first, passing_rest) for c in range(2)]
         diff = keep.tile([N, S], F32, name="diff")
         gated = keep.tile([N, S], F32, name="gated")
         result = keep.tile([N, S], F32, name="result")
@@ -188,7 +188,8 @@ def tile_picked_highway_relu_l_kernel(
 
         def finish(c):
             nc.vector.tensor_tensor(result[:, columns(c)], gated[:, columns(c)], passing[c], ALU.add)
-            nc.sync.dma_start(out=out[:, columns(c)], in_=result[:, columns(c)])
+            queue = nc.scalar if c % 2 else nc.sync
+            queue.dma_start(out=out[:, columns(c)], in_=result[:, columns(c)])
 
         subtract(0)
         subtract(1)

@@ -61,8 +61,8 @@ def tile_picked_highway_relu_l_kernel(
             raw[z, u, first] = keep.tile([P, 2, count], F32, name=raw_tag(z, u, first), align_bytes=64)
             nc.sync.dma_start(out=raw[z, u, first][:], in_=rows[:, 2 * u : 2 * u + 2, first : first + count])
 
-        load_scales(LAYER, w1_scales, nc.gpsimd)
         load_scales(GATE, w2_scales, nc.gpsimd)
+        load_scales(LAYER, w1_scales, nc.gpsimd)
         load_pair(0, 0, 0, T)
         nc.sync.dma_start(offsets[:], offs)
         for z, u in ((0, 1), (1, 0), (1, 1)):
@@ -76,11 +76,11 @@ def tile_picked_highway_relu_l_kernel(
                 in_=words.rearrange("z p b -> p z b")[:, passes, :].bitcast(I32),
             )
 
-        load_words(LAYER, w1_words, slice(0, 1))
+        load_words(GATE, w2_words, slice(0, 1))
         res_sb = keep.tile([P, T], F32, name="res_sb")
         nc.sync.dma_start(out=res_sb[:], in_=res)
-        load_words(GATE, w2_words, slice(0, PASSES))
-        load_words(LAYER, w1_words, slice(1, PASSES))
+        load_words(LAYER, w1_words, slice(0, PASSES))
+        load_words(GATE, w2_words, slice(1, PASSES))
 
         def cast_pair(z, u):
             window = keep.tile([P, T], U32, name="window_%d_%d" % (z, u))
@@ -174,7 +174,8 @@ def tile_picked_highway_relu_l_kernel(
         passing_rest = keep.tile(
             [P, HALF_S], F32, name="passing_rest", tag="picked1", align_bytes=64
         )
-        nc.vector.tensor_copy(passing_rest[:], res_sb[:].indirect(entries(HALF_S, HALF_S)))
+        for c in range(2):
+            nc.vector.tensor_copy(passing_rest[:, columns(c)], res_sb[:].indirect(entries(HALF_S + c * CHUNK, CHUNK)))
         passing = [tile[:, columns(c)] for tile in (passing_first, passing_rest) for c in range(2)]
         diff = keep.tile([N, S], F32, name="diff")
         gated = keep.tile([N, S], F32, name="gated")

@@ -15,15 +15,14 @@ FP8X4 = mybir.dt.float8_e4m3fn_x4
 FP4X4 = mybir.dt.float4_e2m1fn_x4
 ALU = mybir.AluOpType
 SIGMOID = mybir.ActivationFunctionType.Sigmoid
+COPY = mybir.ActivationFunctionType.Copy
 
 P = 128
 K_PASS = 4 * P
 PASSES = K // K_PASS
-HALF_T = T // 2
-HALF_S = S // 2
 CHUNK = 128
 CHUNKS = S // CHUNK
-SCALAR_SHARE = 176
+REST = S - CHUNK
 LAYER, GATE = 0, 1
 
 
@@ -37,168 +36,132 @@ def tile_picked_highway_relu_l_kernel(
 
         offsets = keep.tile([P, S // 16], U16, name="offsets")
 
-        w_scales = [keep.tile([P, PASSES, N], U8, name="w_scales%d" % w, align_bytes=64) for w in (LAYER, GATE)]
-        for w in (LAYER, GATE):
-            nc.gpsimd.memset(w_scales[w][:].rearrange("p z c -> p (z c)").bitcast(I32), 0)
+        staged = keep.tile([16, 2, PASSES, N], U8, name="staged")
+        for w, source in ((LAYER, w1_scales), (GATE, w2_scales)):
+            nc.scalar.dma_start(
+                out=staged[:, w, :, :].bitcast(I32), in_=source.rearrange("z q c -> q z c").bitcast(I32)
+            )
+        w_scales = keep.tile([P, 2, PASSES, N], U8, name="w_scales", align_bytes=64)
+        nc.gpsimd.memset(w_scales[:].rearrange("p w z c -> p (w z c)").bitcast(I32), 0)
+
+        def move_scales():
+            for q in range(4):
+                nc.sync.dma_start(
+                    out=w_scales[32 * q : 32 * q + 4].rearrange("p w z c -> p (w z c)").bitcast(I32),
+                    in_=staged[4 * q : 4 * q + 4].rearrange("p w z c -> p (w z c)").bitcast(I32),
+                )
+
+        w_words = []
+        for w, source in ((LAYER, w1_words), (GATE, w2_words)):
+            w_words.append(keep.tile([P, PASSES, 2 * N], U8, name="w_words%d" % w, align_bytes=64))
+            nc.scalar.dma_start(out=w_words[w][:].bitcast(I32), in_=source.rearrange("z p b -> p z b").bitcast(I32))
 
         warm = keep.tile([P, 8], F32, name="warm")
         warm_out = keep.tile([P, 8], F32, name="warm_out")
         nc.vector.memset(warm[:], 0.0)
         nc.scalar.activation(warm_out[:], warm[:], SIGMOID)
 
-        def load_scales(w, scales, queue):
-            rows = scales.rearrange("z (q r) c -> r q z c", r=4)
-            for r in range(4):
-                queue.dma_start(out=w_scales[w][r:P:32, :, :].bitcast(I32), in_=rows[r].bitcast(I32))
+        rows = {}
 
-        raw = {}
+        def load_row(z, t):
+            rows[z, t] = keep.tile([P, T], F32, name="row_%d_%d" % (z, t))
+            source = xT[K_PASS * z : K_PASS * (z + 1), :].rearrange("(p t) c -> p t c", t=4)
+            nc.sync.dma_start(out=rows[z, t][:], in_=source[:, t, :])
 
-        def raw_tag(z, u, first):
-            return "raw_%d_%d_%d" % (z, u, first)
-
-        def load_pair(z, u, first, count):
-            rows = xT[K_PASS * z : K_PASS * (z + 1), :].rearrange("(p t) c -> p t c", t=4)
-            raw[z, u, first] = keep.tile([P, 2, count], F32, name=raw_tag(z, u, first), align_bytes=64)
-            nc.sync.dma_start(out=raw[z, u, first][:], in_=rows[:, 2 * u : 2 * u + 2, first : first + count])
-
-        load_scales(GATE, w2_scales, nc.gpsimd)
-        load_scales(LAYER, w1_scales, nc.gpsimd)
-        load_pair(0, 0, 0, T)
+        load_row(0, 0)
         nc.sync.dma_start(offsets[:], offs)
-        for z, u in ((0, 1), (1, 0), (1, 1)):
-            load_pair(z, u, 0, HALF_T)
-            load_pair(z, u, HALF_T, HALF_T)
-        w_words = [keep.tile([P, PASSES, 2 * N], U8, name="w_words%d" % w, align_bytes=64) for w in (LAYER, GATE)]
-
-        def load_words(w, words, passes):
-            nc.sync.dma_start(
-                out=w_words[w][:, passes, :].bitcast(I32),
-                in_=words.rearrange("z p b -> p z b")[:, passes, :].bitcast(I32),
-            )
-
-        load_words(GATE, w2_words, slice(0, 1))
+        for t in range(1, 4):
+            load_row(0, t)
+        load_row(1, 0)
+        move_scales()
+        for t in range(1, 4):
+            load_row(1, t)
         res_sb = keep.tile([P, T], F32, name="res_sb")
         nc.sync.dma_start(out=res_sb[:], in_=res)
-        load_words(LAYER, w1_words, slice(0, PASSES))
-        load_words(GATE, w2_words, slice(1, PASSES))
-
-        def cast_pair(z, u):
-            window = keep.tile([P, T], U32, name="window_%d_%d" % (z, u))
-            values = window[:].bitcast(BF16).rearrange("p (c e) -> p c e", e=2)
-            if (z, u, HALF_T) in raw:
-                first, share = HALF_T, SCALAR_SHARE
-                nc.scalar.copy(values[:, 0:HALF_T, :], raw[z, u, 0][:].rearrange("p e c -> p c e"))
-            else:
-                first, share = 0, 2 * SCALAR_SHARE
-            shared = raw[z, u, first][:].rearrange("p e c -> p c e")
-            nc.scalar.copy(values[:, first : first + share, :], shared[:, 0:share, :])
-            nc.vector.tensor_copy(values[:, first + share :, :], shared[:, share:, :])
-            return window
 
         def entries(first, count):
             return offsets[:, first // 16 : (first + count) // 16]
 
-        def gather_pair(window, picked, count):
-            for first in range(0, S, count):
-                nc.vector.tensor_copy(picked[:, first : first + count], window[:].indirect(entries(first, count)))
+        woven = {}
+        codes, scales = {}, {}
+        for z in range(PASSES):
+            for c in range(CHUNKS):
+                woven[z, c] = keep.tile([P, CHUNK, 4], BF16, name="woven_%d_%d" % (z, c), align_bytes=64)
+                codes[z, c] = keep.tile([P, CHUNK], U32, name="codes_%d_%d" % (z, c), align_bytes=64)
+                scales[z, c] = keep.tile([P, CHUNK], U8, name="scales_%d_%d" % (z, c), align_bytes=64)
 
-        def weave(copy, word_dtype, woven, picked):
-            copy(
-                woven[:].bitcast(word_dtype).rearrange("p (c u) -> p c u", u=2),
-                picked.bitcast(word_dtype).rearrange("p u c -> p c u"),
+        planes = {}
+
+        def gather_row(z, t, pieces):
+            u, e = divmod(t, 2)
+            if e == 0:
+                planes[z, u] = keep.tile([P, 2, REST], BF16, name="planes_%d_%d" % (z, u))
+            nc.vector.tensor_copy(woven[z, 0][:, :, t], rows[z, t][:].indirect(entries(0, CHUNK)))
+            width = REST // pieces
+            for first in range(0, REST, width):
+                nc.scalar.activation(
+                    planes[z, u][:, e, first : first + width],
+                    rows[z, t][:].indirect(entries(CHUNK + first, width)),
+                    COPY,
+                )
+
+        def place(z, u, c):
+            nc.vector.tensor_copy(
+                woven[z, c][:, :, 2 * u : 2 * u + 2],
+                planes[z, u][:, :, (c - 1) * CHUNK : c * CHUNK].rearrange("p e c -> p c e"),
             )
 
-        picked0 = keep.tile([P, 2, S], U32, name="picked0")
-        for u in range(2):
-            gather_pair(cast_pair(0, u), picked0[:, u, :], S if u == 0 else HALF_S)
-        woven0 = [keep.tile([P, 4 * HALF_S], BF16, name="woven0_0", align_bytes=64)]
-        weave(nc.vector.tensor_copy, I32, woven0[0], picked0[:, :, 0:HALF_S])
-
-        picked1 = keep.tile([P, 2, S], U32, name="picked1", align_bytes=64)
-        codes0, scales0 = [], []
-        for u in range(2):
-            window = cast_pair(1, u)
-            codes0.append(keep.tile([P, HALF_S], U32, name="codes0_%d" % u, tag=raw_tag(1, u, 0), align_bytes=64))
-            scales0.append(keep.tile([P, HALF_S], U8, name="scales0_%d" % u, align_bytes=64))
-            nc.vector.quantize_mx(out=codes0[u][:].bitcast(FP8X4), scales=scales0[u][:], in_=woven0[u][:])
-            gather_pair(window, picked1[:, u, :], S if u == 0 else CHUNK)
-            if u == 0:
-                woven0.append(
-                    keep.tile([P, 4 * HALF_S], BF16, name="woven0_1", tag=raw_tag(1, 0, HALF_T), align_bytes=64)
-                )
-                weave(nc.scalar.copy, U32, woven0[1], picked0[:, :, HALF_S:S])
-
-        passing_first = keep.tile([P, HALF_S], F32, name="passing_first", tag=raw_tag(1, 1, HALF_T), align_bytes=64)
-        nc.vector.tensor_copy(passing_first[:], res_sb[:].indirect(entries(0, HALF_S)))
-        codes1_all = keep.tile([P, S], U32, name="codes1", align_bytes=64)
-        codes1, scales1 = [], []
-        for c in range(CHUNKS):
-            woven1 = keep.tile([P, 4 * CHUNK], BF16, name="woven1_%d" % c, align_bytes=64)
-            weave(nc.scalar.copy, U32, woven1, picked1[:, :, c * CHUNK : (c + 1) * CHUNK])
-            codes1.append(codes1_all[:, c * CHUNK : (c + 1) * CHUNK])
-            scales1.append(keep.tile([P, CHUNK], U8, name="scales1_%d" % c, align_bytes=64))
-            nc.vector.quantize_mx(out=codes1[c].bitcast(FP8X4), scales=scales1[c][:], in_=woven1[:])
+        def quantise(z, c):
+            nc.vector.quantize_mx(
+                out=codes[z, c][:].bitcast(FP8X4),
+                scales=scales[z, c][:],
+                in_=woven[z, c][:].rearrange("p c t -> p (c t)"),
+            )
 
         sums = {}
 
         def product(w, c, z):
             if z == 0:
-                half, first = divmod(c * CHUNK, HALF_S)
-                codes, scales = codes0[half][:, first : first + CHUNK], scales0[half][:, first : first + CHUNK]
-            else:
-                codes, scales = codes1[c], scales1[c][:]
+                sums[w, c] = psum.tile([N, CHUNK], F32, name="sums_%d_%d" % (w, c))
             nc.tensor.matmul_mx(
                 out=sums[w, c][:],
                 lhsT=w_words[w][:, z, :].bitcast(FP4X4),
-                lhsT_scale=w_scales[w][:, z, :],
-                rhs=codes.bitcast(FP8X4),
-                rhs_scale=scales,
+                lhsT_scale=w_scales[:, w, z, :],
+                rhs=codes[z, c][:].bitcast(FP8X4),
+                rhs_scale=scales[z, c][:],
                 start=(z == 0),
                 stop=(z == PASSES - 1),
             )
 
-        for w in (LAYER, GATE):
+        for z in range(PASSES):
+            gather_row(z, 0, 1)
+            gather_row(z, 1, 1)
+            for c in range(1, CHUNKS):
+                place(z, 0, c)
+            gather_row(z, 2, 1)
+            gather_row(z, 3, 1 if z == 0 else CHUNKS - 1)
+            for c in range(1, CHUNKS):
+                place(z, 1, c)
+                quantise(z, c - 1)
+            quantise(z, CHUNKS - 1)
             for c in range(CHUNKS):
-                sums[w, c] = psum.tile([N, CHUNK], F32, name="sums_%d_%d" % (w, c))
-                product(w, c, 0)
+                product(GATE, c, z)
+                product(LAYER, c, z)
+
+        passing = keep.tile([N, S], F32, name="passing")
         gate = keep.tile([N, S], F32, name="gate")
-
-        def columns(c, chunks=1):
-            return slice(c * CHUNK, (c + chunks) * CHUNK)
-
-        for c in range(CHUNKS):
-            product(LAYER, c, 1)
-            product(GATE, c, 1)
-            nc.scalar.activation(gate[:, columns(c)], sums[GATE, c][:], SIGMOID)
-
-        passing_rest = keep.tile(
-            [P, HALF_S], F32, name="passing_rest", tag="picked1", align_bytes=64
-        )
-        for c in range(2):
-            nc.vector.tensor_copy(passing_rest[:, columns(c)], res_sb[:].indirect(entries(HALF_S + c * CHUNK, CHUNK)))
-        passing = [tile[:, columns(c)] for tile in (passing_first, passing_rest) for c in range(2)]
-        diff = keep.tile([N, S], F32, name="diff")
-        gated = keep.tile([N, S], F32, name="gated")
+        kept = keep.tile([N, S], F32, name="kept")
+        passed = keep.tile([N, S], F32, name="passed")
         result = keep.tile([N, S], F32, name="result")
 
-        def subtract(c):
-            nc.vector.scalar_tensor_tensor(diff[:, columns(c)], sums[LAYER, c][:], 0.0, passing[c], ALU.max, ALU.subtract)
-
-        def multiply(cols):
-            nc.vector.tensor_tensor(gated[:, cols], diff[:, cols], gate[:, cols], ALU.mult)
-
-        def finish(c):
-            nc.vector.tensor_tensor(result[:, columns(c)], gated[:, columns(c)], passing[c], ALU.add)
-            queue = nc.scalar if c % 2 else nc.sync
-            queue.dma_start(out=out[:, columns(c)], in_=result[:, columns(c)])
-
-        subtract(0)
-        subtract(1)
-        subtract(2)
-        subtract(3)
         for c in range(CHUNKS):
-            multiply(columns(c))
-        finish(0)
-        finish(1)
-        finish(2)
-        finish(3)
+            cols = slice(c * CHUNK, (c + 1) * CHUNK)
+            nc.scalar.activation(passing[:, cols], res_sb[:].indirect(entries(c * CHUNK, CHUNK)), COPY)
+            nc.scalar.activation(gate[:, cols], sums[GATE, c][:], SIGMOID)
+        for c in range(CHUNKS):
+            cols = slice(c * CHUNK, (c + 1) * CHUNK)
+            nc.vector.scalar_tensor_tensor(kept[:, cols], sums[LAYER, c][:], 0.0, gate[:, cols], ALU.max, ALU.mult)
+            nc.vector.scalar_tensor_tensor(passed[:, cols], gate[:, cols], 1.0, passing[:, cols], ALU.subtract, ALU.mult)
+            nc.vector.tensor_tensor(result[:, cols], kept[:, cols], passed[:, cols], ALU.subtract)
+            queue = nc.scalar if c % 2 else nc.sync
+            queue.dma_start(out=out[:, cols], in_=result[:, cols])

@@ -51,10 +51,14 @@ def tile_picked_highway_relu_l_kernel(
                     in_=staged[4 * q : 4 * q + 4].rearrange("p w z c -> p (w z c)").bitcast(I32),
                 )
 
-        w_words = []
-        for w, source in ((LAYER, w1_words), (GATE, w2_words)):
-            w_words.append(keep.tile([P, PASSES, 2 * N], U8, name="w_words%d" % w, align_bytes=64))
-            nc.scalar.dma_start(out=w_words[w][:].bitcast(I32), in_=source.rearrange("z p b -> p z b").bitcast(I32))
+        w_words = {}
+
+        def load_words(z, queue):
+            for w, source in ((LAYER, w1_words), (GATE, w2_words)):
+                w_words[w, z] = keep.tile([P, 2 * N], U8, name="w_words_%d_%d" % (w, z), align_bytes=64)
+                queue.dma_start(out=w_words[w, z][:].bitcast(I32), in_=source[z].bitcast(I32))
+
+        load_words(0, nc.scalar)
 
         warm = keep.tile([P, 8], F32, name="warm")
         warm_out = keep.tile([P, 8], F32, name="warm_out")
@@ -78,17 +82,14 @@ def tile_picked_highway_relu_l_kernel(
             load_row(1, t)
         res_sb = keep.tile([P, T], F32, name="res_sb")
         nc.sync.dma_start(out=res_sb[:], in_=res)
+        load_words(1, nc.sync)
 
         def entries(first, count):
             return offsets[:, first // 16 : (first + count) // 16]
 
-        woven = {}
-        codes, scales = {}, {}
-        for z in range(PASSES):
-            for c in range(CHUNKS):
-                woven[z, c] = keep.tile([P, CHUNK, 4], BF16, name="woven_%d_%d" % (z, c), align_bytes=64)
-                codes[z, c] = keep.tile([P, CHUNK], U32, name="codes_%d_%d" % (z, c), align_bytes=64)
-                scales[z, c] = keep.tile([P, CHUNK], U8, name="scales_%d_%d" % (z, c), align_bytes=64)
+        woven = [keep.tile([P, S, 4], BF16, name="woven%d" % z, align_bytes=64) for z in range(PASSES)]
+        codes = [keep.tile([P, S], U32, name="codes%d" % z, align_bytes=64) for z in range(PASSES)]
+        scales = [keep.tile([P, S], U8, name="scales%d" % z, align_bytes=64) for z in range(PASSES)]
 
         planes = {}
 
@@ -96,7 +97,7 @@ def tile_picked_highway_relu_l_kernel(
             u, e = divmod(t, 2)
             if e == 0:
                 planes[z, u] = keep.tile([P, 2, REST], BF16, name="planes_%d_%d" % (z, u))
-            nc.vector.tensor_copy(woven[z, 0][:, :, t], rows[z, t][:].indirect(entries(0, CHUNK)))
+            nc.vector.tensor_copy(woven[z][:, 0:CHUNK, t], rows[z, t][:].indirect(entries(0, CHUNK)))
             width = REST // pieces
             for first in range(0, REST, width):
                 nc.scalar.activation(
@@ -105,17 +106,17 @@ def tile_picked_highway_relu_l_kernel(
                     COPY,
                 )
 
-        def place(z, u, c):
+        def place(z, u, first, count):
             nc.vector.tensor_copy(
-                woven[z, c][:, :, 2 * u : 2 * u + 2],
-                planes[z, u][:, :, (c - 1) * CHUNK : c * CHUNK].rearrange("p e c -> p c e"),
+                woven[z][:, first : first + count, 2 * u : 2 * u + 2],
+                planes[z, u][:, :, first - CHUNK : first - CHUNK + count].rearrange("p e c -> p c e"),
             )
 
-        def quantise(z, c):
+        def quantise(z, first, count):
             nc.vector.quantize_mx(
-                out=codes[z, c][:].bitcast(FP8X4),
-                scales=scales[z, c][:],
-                in_=woven[z, c][:].rearrange("p c t -> p (c t)"),
+                out=codes[z][:, first : first + count].bitcast(FP8X4),
+                scales=scales[z][:, first : first + count],
+                in_=woven[z][:, first : first + count, :].rearrange("p c t -> p (c t)"),
             )
 
         sums = {}
@@ -125,10 +126,10 @@ def tile_picked_highway_relu_l_kernel(
                 sums[w, c] = psum.tile([N, CHUNK], F32, name="sums_%d_%d" % (w, c))
             nc.tensor.matmul_mx(
                 out=sums[w, c][:],
-                lhsT=w_words[w][:, z, :].bitcast(FP4X4),
+                lhsT=w_words[w, z][:].bitcast(FP4X4),
                 lhsT_scale=w_scales[:, w, z, :],
-                rhs=codes[z, c][:].bitcast(FP8X4),
-                rhs_scale=scales[z, c][:],
+                rhs=codes[z][:, c * CHUNK : (c + 1) * CHUNK].bitcast(FP8X4),
+                rhs_scale=scales[z][:, c * CHUNK : (c + 1) * CHUNK],
                 start=(z == 0),
                 stop=(z == PASSES - 1),
             )
@@ -136,32 +137,46 @@ def tile_picked_highway_relu_l_kernel(
         for z in range(PASSES):
             gather_row(z, 0, 1)
             gather_row(z, 1, 1)
-            for c in range(1, CHUNKS):
-                place(z, 0, c)
+            place(z, 0, CHUNK, REST)
             gather_row(z, 2, 1)
             gather_row(z, 3, 1 if z == 0 else CHUNKS - 1)
-            for c in range(1, CHUNKS):
-                place(z, 1, c)
-                quantise(z, c - 1)
-            quantise(z, CHUNKS - 1)
+            if z == 0:
+                place(z, 1, CHUNK, REST)
+                quantise(z, 0, S)
+            else:
+                for c in range(1, CHUNKS):
+                    place(z, 1, c * CHUNK, CHUNK)
+                    quantise(z, (c - 1) * CHUNK, CHUNK)
+                quantise(z, REST, CHUNK)
             for c in range(CHUNKS):
-                product(GATE, c, z)
                 product(LAYER, c, z)
+                product(GATE, c, z)
 
         passing = keep.tile([N, S], F32, name="passing")
         gate = keep.tile([N, S], F32, name="gate")
-        kept = keep.tile([N, S], F32, name="kept")
-        passed = keep.tile([N, S], F32, name="passed")
+        diff = keep.tile([N, S], F32, name="diff")
+        gated = keep.tile([N, S], F32, name="gated")
         result = keep.tile([N, S], F32, name="result")
 
+        def columns(c):
+            return slice(c * CHUNK, (c + 1) * CHUNK)
+
         for c in range(CHUNKS):
-            cols = slice(c * CHUNK, (c + 1) * CHUNK)
-            nc.scalar.activation(passing[:, cols], res_sb[:].indirect(entries(c * CHUNK, CHUNK)), COPY)
-            nc.scalar.activation(gate[:, cols], sums[GATE, c][:], SIGMOID)
+            nc.scalar.activation(passing[:, columns(c)], res_sb[:].indirect(entries(c * CHUNK, CHUNK)), COPY)
         for c in range(CHUNKS):
-            cols = slice(c * CHUNK, (c + 1) * CHUNK)
-            nc.vector.scalar_tensor_tensor(kept[:, cols], sums[LAYER, c][:], 0.0, gate[:, cols], ALU.max, ALU.mult)
-            nc.vector.scalar_tensor_tensor(passed[:, cols], gate[:, cols], 1.0, passing[:, cols], ALU.subtract, ALU.mult)
-            nc.vector.tensor_tensor(result[:, cols], kept[:, cols], passed[:, cols], ALU.subtract)
+            nc.scalar.activation(gate[:, columns(c)], sums[GATE, c][:], SIGMOID)
+        for c in range(CHUNKS):
+            nc.vector.scalar_tensor_tensor(
+                diff[:, columns(c)], sums[LAYER, c][:], 0.0, passing[:, columns(c)], ALU.max, ALU.subtract
+            )
+
+        def finish(c):
+            nc.vector.tensor_tensor(result[:, columns(c)], gated[:, columns(c)], passing[:, columns(c)], ALU.add)
             queue = nc.scalar if c % 2 else nc.sync
-            queue.dma_start(out=out[:, cols], in_=result[:, cols])
+            queue.dma_start(out=out[:, columns(c)], in_=result[:, columns(c)])
+
+        for c in range(CHUNKS):
+            nc.vector.tensor_tensor(gated[:, columns(c)], diff[:, columns(c)], gate[:, columns(c)], ALU.mult)
+            if c > 0:
+                finish(c - 1)
+        finish(CHUNKS - 1)

@@ -58,7 +58,6 @@ def tile_picked_highway_relu_l_kernel(
                 w_words[w, z] = keep.tile([P, 2 * N], U8, name="w_words_%d_%d" % (w, z), align_bytes=64)
                 queue.dma_start(out=w_words[w, z][:].bitcast(I32), in_=source[z].bitcast(I32))
 
-        load_words(0, nc.scalar)
 
         warm = keep.tile([P, 8], F32, name="warm")
         warm_out = keep.tile([P, 8], F32, name="warm_out")
@@ -80,6 +79,7 @@ def tile_picked_highway_relu_l_kernel(
         move_scales()
         for t in range(1, 4):
             load_row(1, t)
+        load_words(0, nc.sync)
         res_sb = keep.tile([P, T], F32, name="res_sb")
         nc.sync.dma_start(out=res_sb[:], in_=res)
         load_words(1, nc.sync)
@@ -172,7 +172,7 @@ def tile_picked_highway_relu_l_kernel(
 
         def finish(c):
             nc.vector.tensor_tensor(result[:, columns(c)], gated[:, columns(c)], passing[:, columns(c)], ALU.add)
-            queue = nc.scalar if c % 2 else nc.sync
+            queue = nc.sync if c % 2 else nc.scalar
             queue.dma_start(out=out[:, columns(c)], in_=result[:, columns(c)])
 
         for c in range(CHUNKS):

@@ -161,8 +161,8 @@ def tile_picked_highway_relu_l_kernel(
         def columns(c):
             return slice(c * CHUNK, (c + 1) * CHUNK)
 
-        for c in range(CHUNKS):
-            nc.scalar.activation(passing[:, columns(c)], res_sb[:].indirect(entries(c * CHUNK, CHUNK)), COPY)
+        for first in range(0, S, S // 2):
+            nc.scalar.activation(passing[:, first : first + S // 2], res_sb[:].indirect(entries(first, S // 2)), COPY)
         for c in range(CHUNKS):
             nc.scalar.activation(gate[:, columns(c)], sums[GATE, c][:], SIGMOID)
         for c in range(CHUNKS):

@@ -23,6 +23,7 @@ PASSES = K // K_PASS
 CHUNK = 128
 CHUNKS = S // CHUNK
 REST = S - CHUNK
+HALF = S // 2
 LAYER, GATE = 0, 1
 
 
@@ -93,16 +94,15 @@ def tile_picked_highway_relu_l_kernel(
 
         planes = {}
 
-        def gather_row(z, t, pieces):
+        def gather_row(z, t, cuts):
             u, e = divmod(t, 2)
             if e == 0:
                 planes[z, u] = keep.tile([P, 2, REST], BF16, name="planes_%d_%d" % (z, u))
             nc.vector.tensor_copy(woven[z][:, 0:CHUNK, t], rows[z, t][:].indirect(entries(0, CHUNK)))
-            width = REST // pieces
-            for first in range(0, REST, width):
+            for first, last in zip((CHUNK,) + cuts, cuts + (S,)):
                 nc.scalar.activation(
-                    planes[z, u][:, e, first : first + width],
-                    rows[z, t][:].indirect(entries(CHUNK + first, width)),
+                    planes[z, u][:, e, first - CHUNK : last - CHUNK],
+                    rows[z, t][:].indirect(entries(first, last - first)),
                     COPY,
                 )
 
@@ -135,15 +135,22 @@ def tile_picked_highway_relu_l_kernel(
             )
 
         for z in range(PASSES):
-            gather_row(z, 0, 1)
-            gather_row(z, 1, 1)
-            place(z, 0, CHUNK, REST)
-            gather_row(z, 2, 1)
-            gather_row(z, 3, 1 if z == 0 else CHUNKS - 1)
+            gather_row(z, 0, ())
             if z == 0:
-                place(z, 1, CHUNK, REST)
-                quantise(z, 0, S)
+                gather_row(z, 1, ())
+                place(z, 0, CHUNK, REST)
+                gather_row(z, 2, ())
+                gather_row(z, 3, (HALF,))
+                place(z, 1, CHUNK, CHUNK)
+                quantise(z, 0, HALF)
+                place(z, 1, HALF, HALF)
+                quantise(z, HALF, HALF)
             else:
+                gather_row(z, 1, (HALF,))
+                place(z, 0, CHUNK, CHUNK)
+                place(z, 0, HALF, HALF)
+                gather_row(z, 2, ())
+                gather_row(z, 3, (2 * CHUNK, 3 * CHUNK))
                 for c in range(1, CHUNKS):
                     place(z, 1, c * CHUNK, CHUNK)
                     quantise(z, (c - 1) * CHUNK, CHUNK)

@@ -24,6 +24,7 @@ CHUNK = 128
 CHUNKS = S // CHUNK
 REST = S - CHUNK
 HALF = S // 2
+SHARE = 160
 LAYER, GATE = 0, 1
 
 
@@ -94,12 +95,12 @@ def tile_picked_highway_relu_l_kernel(
 
         planes = {}
 
-        def gather_row(z, t, cuts):
+        def gather_row(z, t, cuts, share=CHUNK):
             u, e = divmod(t, 2)
             if e == 0:
                 planes[z, u] = keep.tile([P, 2, REST], BF16, name="planes_%d_%d" % (z, u))
-            nc.vector.tensor_copy(woven[z][:, 0:CHUNK, t], rows[z, t][:].indirect(entries(0, CHUNK)))
-            for first, last in zip((CHUNK,) + cuts, cuts + (S,)):
+            nc.vector.tensor_copy(woven[z][:, 0:share, t], rows[z, t][:].indirect(entries(0, share)))
+            for first, last in zip((share,) + cuts, cuts + (S,)):
                 nc.scalar.activation(
                     planes[z, u][:, e, first - CHUNK : last - CHUNK],
                     rows[z, t][:].indirect(entries(first, last - first)),
@@ -135,19 +136,19 @@ def tile_picked_highway_relu_l_kernel(
             )
 
         for z in range(PASSES):
-            gather_row(z, 0, ())
+            gather_row(z, 0, (), SHARE)
             if z == 0:
-                gather_row(z, 1, ())
-                place(z, 0, CHUNK, REST)
-                gather_row(z, 2, ())
-                gather_row(z, 3, (HALF,))
-                place(z, 1, CHUNK, CHUNK)
+                gather_row(z, 1, (), SHARE)
+                place(z, 0, SHARE, S - SHARE)
+                gather_row(z, 2, (), SHARE)
+                gather_row(z, 3, (HALF,), SHARE)
+                place(z, 1, SHARE, HALF - SHARE)
                 quantise(z, 0, HALF)
                 place(z, 1, HALF, HALF)
                 quantise(z, HALF, HALF)
             else:
-                gather_row(z, 1, (HALF,))
-                place(z, 0, CHUNK, CHUNK)
+                gather_row(z, 1, (HALF,), SHARE)
+                place(z, 0, SHARE, HALF - SHARE)
                 place(z, 0, HALF, HALF)
                 gather_row(z, 2, ())
                 gather_row(z, 3, (2 * CHUNK, 3 * CHUNK))

from contextlib import ExitStack

import concourse.mybir as mybir

K, T, S, N = 1024, 1024, 512, 128
FLOPS = 2 * 2 * K * S * N

F32 = mybir.dt.float32
BF16 = mybir.dt.bfloat16
I32 = mybir.dt.int32
U32 = mybir.dt.uint32
U16 = mybir.dt.uint16
U8 = mybir.dt.uint8
FP8X4 = mybir.dt.float8_e4m3fn_x4
FP4X4 = mybir.dt.float4_e2m1fn_x4
ALU = mybir.AluOpType
SIGMOID = mybir.ActivationFunctionType.Sigmoid
COPY = mybir.ActivationFunctionType.Copy

P = 128
K_PASS = 4 * P
PASSES = K // K_PASS
CHUNK = 128
CHUNKS = S // CHUNK
REST = S - CHUNK
HALF = S // 2
SHARE = 160
LAYER, GATE = 0, 1


def tile_picked_highway_relu_l_kernel(
    tc, xT, res, w1_words, w1_scales, w2_words, w2_scales, offs, out
):
    nc = tc.nc
    with ExitStack() as ctx:
        keep = ctx.enter_context(tc.tile_pool(name="keep", bufs=1))
        psum = ctx.enter_context(tc.psum_pool(name="psum", bufs=1))

        offsets = keep.tile([P, S // 16], U16, name="offsets")

        staged = keep.tile([16, 2, PASSES, N], U8, name="staged")
        for w, source in ((LAYER, w1_scales), (GATE, w2_scales)):
            nc.scalar.dma_start(
                out=staged[:, w, :, :].bitcast(I32), in_=source.rearrange("z q c -> q z c").bitcast(I32)
            )
        w_scales = keep.tile([P, 2, PASSES, N], U8, name="w_scales", align_bytes=64)
        nc.gpsimd.memset(w_scales[:].rearrange("p w z c -> p (w z c)").bitcast(I32), 0)

        def move_scales():
            for q in range(4):
                nc.sync.dma_start(
                    out=w_scales[32 * q : 32 * q + 4].rearrange("p w z c -> p (w z c)").bitcast(I32),
                    in_=staged[4 * q : 4 * q + 4].rearrange("p w z c -> p (w z c)").bitcast(I32),
                )

        w_words = {}

        def load_words(z, queue):
            for w, source in ((LAYER, w1_words), (GATE, w2_words)):
                w_words[w, z] = keep.tile([P, 2 * N], U8, name="w_words_%d_%d" % (w, z), align_bytes=64)
                queue.dma_start(out=w_words[w, z][:].bitcast(I32), in_=source[z].bitcast(I32))


        warm = keep.tile([P, 8], F32, name="warm")
        warm_out = keep.tile([P, 8], F32, name="warm_out")
        nc.vector.memset(warm[:], 0.0)
        nc.scalar.activation(warm_out[:], warm[:], SIGMOID)

        rows = {}

        def load_row(z, t):
            rows[z, t] = keep.tile([P, T], F32, name="row_%d_%d" % (z, t))
            source = xT[K_PASS * z : K_PASS * (z + 1), :].rearrange("(p t) c -> p t c", t=4)
            nc.sync.dma_start(out=rows[z, t][:], in_=source[:, t, :])

        load_row(0, 0)
        nc.sync.dma_start(offsets[:], offs)
        for t in range(1, 4):
            load_row(0, t)
        load_row(1, 0)
        move_scales()
        for t in range(1, 4):
            load_row(1, t)
        load_words(0, nc.sync)
        res_sb = keep.tile([P, T], F32, name="res_sb")
        nc.sync.dma_start(out=res_sb[:], in_=res)
        load_words(1, nc.sync)

        def entries(first, count):
            return offsets[:, first // 16 : (first + count) // 16]

        woven = [keep.tile([P, S, 4], BF16, name="woven%d" % z, align_bytes=64) for z in range(PASSES)]
        codes = [keep.tile([P, S], U32, name="codes%d" % z, align_bytes=64) for z in range(PASSES)]
        scales = [keep.tile([P, S], U8, name="scales%d" % z, align_bytes=64) for z in range(PASSES)]

        planes = {}

        def gather_row(z, t, cuts, share=CHUNK):
            u, e = divmod(t, 2)
            if e == 0:
                planes[z, u] = keep.tile([P, 2, REST], BF16, name="planes_%d_%d" % (z, u))
            nc.vector.tensor_copy(woven[z][:, 0:share, t], rows[z, t][:].indirect(entries(0, share)))
            for first, last in zip((share,) + cuts, cuts + (S,)):
                nc.scalar.activation(
                    planes[z, u][:, e, first - CHUNK : last - CHUNK],
                    rows[z, t][:].indirect(entries(first, last - first)),
                    COPY,
                )

        def place(z, u, first, count):
            nc.vector.tensor_copy(
                woven[z][:, first : first + count, 2 * u : 2 * u + 2],
                planes[z, u][:, :, first - CHUNK : first - CHUNK + count].rearrange("p e c -> p c e"),
            )

        def quantise(z, first, count):
            nc.vector.quantize_mx(
                out=codes[z][:, first : first + count].bitcast(FP8X4),
                scales=scales[z][:, first : first + count],
                in_=woven[z][:, first : first + count, :].rearrange("p c t -> p (c t)"),
            )

        sums = {}

        def product(w, c, z):
            if z == 0:
                sums[w, c] = psum.tile([N, CHUNK], F32, name="sums_%d_%d" % (w, c))
            nc.tensor.matmul_mx(
                out=sums[w, c][:],
                lhsT=w_words[w, z][:].bitcast(FP4X4),
                lhsT_scale=w_scales[:, w, z, :],
                rhs=codes[z][:, c * CHUNK : (c + 1) * CHUNK].bitcast(FP8X4),
                rhs_scale=scales[z][:, c * CHUNK : (c + 1) * CHUNK],
                start=(z == 0),
                stop=(z == PASSES - 1),
            )

        for z in range(PASSES):
            gather_row(z, 0, (), SHARE)
            if z == 0:
                gather_row(z, 1, (), SHARE)
                place(z, 0, SHARE, S - SHARE)
                gather_row(z, 2, (), SHARE)
                gather_row(z, 3, (HALF,), SHARE)
                place(z, 1, SHARE, HALF - SHARE)
                quantise(z, 0, HALF)
                place(z, 1, HALF, HALF)
                quantise(z, HALF, HALF)
            else:
                gather_row(z, 1, (HALF,), SHARE)
                place(z, 0, SHARE, HALF - SHARE)
                place(z, 0, HALF, HALF)
                gather_row(z, 2, ())
                gather_row(z, 3, (2 * CHUNK, 3 * CHUNK))
                for c in range(1, CHUNKS):
                    place(z, 1, c * CHUNK, CHUNK)
                    quantise(z, (c - 1) * CHUNK, CHUNK)
                quantise(z, REST, CHUNK)
            for c in range(CHUNKS):
                product(LAYER, c, z)
                product(GATE, c, z)

        passing = keep.tile([N, S], F32, name="passing")
        gate = keep.tile([N, S], F32, name="gate")
        diff = keep.tile([N, S], F32, name="diff")
        gated = keep.tile([N, S], F32, name="gated")
        result = keep.tile([N, S], F32, name="result")

        def columns(c):
            return slice(c * CHUNK, (c + 1) * CHUNK)

        for first in range(0, S, S // 2):
            nc.scalar.activation(passing[:, first : first + S // 2], res_sb[:].indirect(entries(first, S // 2)), COPY)
        for c in range(CHUNKS):
            nc.scalar.activation(gate[:, columns(c)], sums[GATE, c][:], SIGMOID)
        for c in range(CHUNKS):
            nc.vector.scalar_tensor_tensor(
                diff[:, columns(c)], sums[LAYER, c][:], 0.0, passing[:, columns(c)], ALU.max, ALU.subtract
            )

        def finish(c):
            nc.vector.tensor_tensor(result[:, columns(c)], gated[:, columns(c)], passing[:, columns(c)], ALU.add)
            queue = nc.sync if c % 2 else nc.scalar
            queue.dma_start(out=out[:, columns(c)], in_=result[:, columns(c)])

        for c in range(CHUNKS):
            nc.vector.tensor_tensor(gated[:, columns(c)], diff[:, columns(c)], gate[:, columns(c)], ALU.mult)
            if c > 0:
                finish(c - 1)
        finish(CHUNKS - 1)
